import numpy as np
import ml_dtypes


def mxq(x, axis, fmt="e4m3"):
    dtype, down = {"e4m3": (ml_dtypes.float8_e4m3fn, 7), "e5m2": (ml_dtypes.float8_e5m2, 14)}[fmt]
    v = np.moveaxis(np.asarray(x, np.float32).astype(ml_dtypes.bfloat16).astype(np.float64), axis, -1)
    blocks = v.reshape(v.shape[:-1] + (-1, 32))
    amax = np.abs(blocks).max(-1, keepdims=True)
    byte = np.maximum(np.where(amax > 0, np.frexp(amax)[1] - 1 + 127, 0) - down, 1)
    scale = np.exp2(byte - 127.0)
    codes = (blocks / scale).astype(np.float32).astype(dtype).astype(np.float64)
    return np.moveaxis((codes * scale).reshape(v.shape), -1, axis)


WIDE = False


def mx_kscale(k):
    if not WIDE:
        return np.ones(k)
    levels = np.array([10, -10, 5, -5, 0])
    if k % 512:
        return np.exp2(np.random.permutation(np.resize(levels, k // 32))).repeat(32)
    a = np.empty((k // 512, 16))
    for p in range(k // 512):
        a[p, :8] = np.random.permutation(np.resize(levels, 8))
        for g in range(8):
            far = levels[np.abs(levels - a[p, g]) >= 10]
            a[p, g + 8] = far[np.random.randint(len(far))]
    return np.exp2(a.ravel()).repeat(32)


def f64(x):
    return np.asarray(x).astype(np.float64)


def striped(idx):
    return np.tile(idx.reshape(-1, 16).T, (8, 1)).astype(np.uint16)


def unstriped(offs):
    return offs[:16].T.reshape(-1).astype(np.int64)


E2M1 = np.array([0.0, 0.5, 1.0, 1.5, 2.0, 3.0, 4.0, 6.0, -0.0, -0.5, -1.0, -1.5, -2.0, -3.0, -4.0, -6.0])


def pack_weight(w, fmt):
    k, n = w.shape
    w = f64(np.asarray(w, np.float32).astype(ml_dtypes.bfloat16)).reshape(k // 32, 32, n)
    amax = np.abs(w).max(1)
    if fmt == "e4m3":
        byte = np.frexp(amax)[1] - 1 + 127 - 7
    else:
        mant, ex = np.frexp(amax / 6.0)
        byte = np.where(mant > 0.5, ex, ex - 1) + 127
    byte = np.clip(np.where(amax > 0, byte, 1), 1, 254)
    scaled = (w * np.exp2(127.0 - byte)[:, None, :]).reshape(k, n).astype(np.float32)
    by_word = np.ascontiguousarray(scaled.reshape(k // 512, 128, 4, n).transpose(0, 1, 3, 2))
    if fmt == "e4m3":
        words = by_word.astype(ml_dtypes.float8_e4m3fn).view(np.uint8)
    else:
        c = by_word.astype(ml_dtypes.float4_e2m1fn).view(np.uint8) & 0xF
        words = (c[..., 0::2] | (c[..., 1::2] << 4)).reshape(k // 512, 128, 2 * n)
    return np.ascontiguousarray(words), np.ascontiguousarray(byte.astype(np.uint8).reshape(k // 512, 16, n))


def unpack_weight(words, scales, fmt):
    g, _, n = scales.shape
    words = np.ascontiguousarray(words).reshape(g, 128, n, -1)
    if fmt == "e4m3":
        vals = words.view(ml_dtypes.float8_e4m3fn).astype(np.float64)
    else:
        nib = np.empty((g, 128, n, 4), np.uint8)
        nib[..., 0::2] = words & 0xF
        nib[..., 1::2] = words >> 4
        vals = E2M1[nib]
    vals = vals * np.repeat(np.exp2(scales.astype(np.float64) - 127.0), 8, axis=1)[..., None]
    return vals.transpose(0, 1, 3, 2).reshape(g * 512, n)


def relu(v):
    return np.maximum(v, 0.0)


K, T, E, C, H, N = 1024, 512, 8, 128, 512, 128


def by_expert(wq, xq):
    return np.concatenate([wq[e].T @ xq[:, e * C:(e + 1) * C] for e in range(E)], axis=1)


def setup_inputs():
    n = np.random.standard_normal
    s = mx_kscale(K)[:, None]
    u = mx_kscale(H)
    first = np.random.permutation(np.repeat(np.arange(E), T // E))
    second = (first + 1 + np.random.permutation(np.repeat(np.arange(E - 1), -(-T // (E - 1)))[:T])) % E
    while np.bincount(second, minlength=E).max() != T // E:
        load = np.bincount(second, minlength=E); hi, lo = int(load.argmax()), int(load.argmin())
        t = np.flatnonzero((second == hi) & (first != lo))[0]; second[t] = lo
    slot_token = np.empty(E * C, np.int64); pos = np.empty((2, T), np.int64); fill = np.zeros(E, np.int64)
    place = np.stack([np.random.permutation(C) for _ in range(E)])
    for r, deal in enumerate((first, second)):
        for t in np.random.permutation(T):
            e = deal[t]; j = e * C + place[e, fill[e]]; fill[e] += 1; slot_token[j] = t; pos[r, t] = j
    g = np.random.uniform(0.2, 0.8, T)
    w1 = [pack_weight(m, "e2m1") for m in n((E + 1, K, H)) / np.sqrt(K) / s[None]]
    w3 = [pack_weight(m, "e2m1") for m in n((E + 1, K, H)) / np.sqrt(K) / s[None] * u[None, None, :]]
    w2 = [pack_weight(m, "e2m1") for m in n((E + 1, H, N)) / np.sqrt(H) / u[None, :, None]]
    x = pack_weight(n((K, T)) * s, "e4m3")
    return {
        "x_words": x[0],
        "x_scales": x[1],
        "w1_words": np.stack([m[0] for m in w1]),
        "w1_scales": np.stack([m[1] for m in w1]),
        "w3_words": np.stack([m[0] for m in w3]),
        "w3_scales": np.stack([m[1] for m in w3]),
        "w2_words": np.stack([m[0] for m in w2]),
        "w2_scales": np.stack([m[1] for m in w2]),
        "gate": np.stack([np.tile(g, (N, 1)), np.tile(1.0 - g, (N, 1))]).astype(np.float32),
        "offs": striped(slot_token),
        "pos1": striped(pos[0]),
        "pos2": striped(pos[1]),
    }


def reference(x_words, x_scales, w1_words, w1_scales, w3_words, w3_scales, w2_words, w2_scales, gate, offs, pos1, pos2):
    idx = unstriped(offs)
    w1 = np.stack([unpack_weight(w1_words[e], w1_scales[e], "e2m1") for e in range(E + 1)])
    w3 = np.stack([unpack_weight(w3_words[e], w3_scales[e], "e2m1") for e in range(E + 1)])
    w2 = np.stack([unpack_weight(w2_words[e], w2_scales[e], "e2m1") for e in range(E + 1)])
    w1q, w3q, w2q = w1, w3, w2
    xs = unpack_weight(x_words, x_scales, "e4m3")
    hs = relu(w1q[E].T @ xs) * (w3q[E].T @ xs)
    ys = w2q[E].T @ mxq(hs, 0, "e4m3")
    xq = unpack_weight(x_words, x_scales, "e4m3")[:, idx]
    h = relu(by_expert(w1q, xq))
    h = h * by_expert(w3q, xq)
    y = by_expert(w2q, mxq(h, 0, "e4m3"))
    return ys + f64(gate[0]) * y[:, unstriped(pos1)] + f64(gate[1]) * y[:, unstriped(pos2)]

@@ -1,0 +1,224 @@
+from contextlib import ExitStack
+
+import concourse.mybir as mybir
+from concourse.masks import make_identity
+
+K, T, E, C, H, N = 1024, 512, 8, 128, 512, 128
+FLOPS = 2 * (E * C + T) * (2 * K * H + H * N)
+
+F32 = mybir.dt.float32
+BF16 = mybir.dt.bfloat16
+I32 = mybir.dt.int32
+U32 = mybir.dt.uint32
+U16 = mybir.dt.uint16
+U8 = mybir.dt.uint8
+FP8X4 = mybir.dt.float8_e4m3fn_x4
+FP4X4 = mybir.dt.float4_e2m1fn_x4
+MULT = mybir.AluOpType.mult
+ADD = mybir.AluOpType.add
+RELU = mybir.ActivationFunctionType.Relu
+
+P = 128
+PASSES = K // 512
+SLOTS = E * C
+SHARED = E
+GATHER = 256
+HALF = T // 2
+
+
+def load_plane(queue, plane, rows):
+    by_row = rows.rearrange("m (q r) c -> r q m c", r=4)
+    for r in range(4):
+        queue.dma_start(out=plane[r:P:32, :, :].bitcast(I32), in_=by_row[r].bitcast(I32))
+
+
+def tile_moe_shr_glu_relu_kernel(
+    tc, x_words, x_scales, w1_words, w1_scales, w3_words, w3_scales, w2_words, w2_scales, gate, offs, pos1, pos2, out
+):
+    nc = tc.nc
+    with ExitStack() as ctx:
+        keep = ctx.enter_context(tc.tile_pool(name="keep", bufs=1))
+        ring = ctx.enter_context(tc.tile_pool(name="ring", bufs=3))
+        reuse = ctx.enter_context(tc.tile_pool(name="reuse", bufs=1))
+        psum = ctx.enter_context(tc.psum_pool(name="psum", bufs=3))
+        psum_t = ctx.enter_context(tc.psum_pool(name="psum_t", bufs=2))
+
+        offs_t = keep.tile([P, SLOTS // 16], U16, name="offs_t")
+        pos1_t = keep.tile([P, T // 16], U16, name="pos1_t")
+        pos2_t = keep.tile([P, T // 16], U16, name="pos2_t")
+        xw = [keep.tile([P, T], U32, name="xw%d" % o, align_bytes=64) for o in range(PASSES)]
+        xs = keep.tile([P, PASSES, T], U8, name="xs", align_bytes=64)
+        w1 = [keep.tile([P, PASSES, 2 * H], U8, name="w1_%d" % e, align_bytes=64) for e in range(E + 1)]
+        w3 = [keep.tile([P, PASSES, 2 * H], U8, name="w3_%d" % e, align_bytes=64) for e in range(E + 1)]
+        w2 = keep.tile([P, E + 1, 2 * N], U8, name="w2", align_bytes=64)
+        s1_shared = keep.tile([P, PASSES, H], U8, name="s1_shared", align_bytes=64)
+        s3_shared = keep.tile([P, PASSES, H], U8, name="s3_shared", align_bytes=64)
+        s1_routed = keep.tile([P, E * PASSES, H], U8, name="s1_routed", align_bytes=64)
+        s3_routed = keep.tile([P, E * PASSES, H], U8, name="s3_routed", align_bytes=64)
+        s2 = keep.tile([P, E + 1, N], U8, name="s2", align_bytes=64)
+        gate_t = keep.tile([P, 2, T], F32, name="gate_t")
+        ident = keep.tile([P, P], F32, name="ident")
+
+        for plane in (xs, s1_shared, s3_shared, s3_routed):
+            nc.vector.memset(plane[:].bitcast(I32), 0)
+        for plane in (s1_routed, s2):
+            nc.gpsimd.memset(plane[:].bitcast(I32), 0)
+        make_identity(nc, ident[:])
+
+        def load_words(tile, words):
+            nc.sync.dma_start(out=tile[:].bitcast(I32), in_=words.rearrange("s p c -> p s c").bitcast(I32))
+
+        def load_tokens(o):
+            nc.sync.dma_start(out=xw[o][:].bitcast(I32), in_=x_words[o].rearrange("p t r -> p (t r)").bitcast(I32))
+
+        nc.sync.dma_start(offs_t[:], offs)
+        load_tokens(0)
+        load_words(w1[SHARED], w1_words[SHARED])
+        load_tokens(1)
+        load_words(w3[SHARED], w3_words[SHARED])
+        load_plane(nc.sync, xs, x_scales)
+        load_plane(nc.sync, s1_shared, w1_scales[SHARED])
+        load_plane(nc.sync, s3_shared, w3_scales[SHARED])
+        load_plane(nc.sync, s1_routed, w1_scales[0:E].rearrange("e s f c -> (e s) f c"))
+        load_plane(nc.sync, s3_routed, w3_scales[0:E].rearrange("e s f c -> (e s) f c"))
+        load_plane(nc.sync, s2, w2_scales.rearrange("e s f c -> (e s) f c"))
+        for e in range(E):
+            load_words(w1[e], w1_words[e])
+            load_words(w3[e], w3_words[e])
+        load_words(w2, w2_words.rearrange("e s p c -> (e s) p c"))
+        nc.sync.dma_start(pos1_t[:], pos1)
+        nc.sync.dma_start(pos2_t[:], pos2)
+        nc.sync.dma_start(out=gate_t[:], in_=gate.rearrange("r p t -> p r t"))
+
+        gw = {}
+        gs = {}
+        half_region = 2 * H
+        place = {7: 0, 8: 1, 9: 2, 10: 4, 11: 6, 12: 8, 13: 10, 14: 12, 15: 14}
+
+        def gathered(index, dtype):
+            name = "gathered%d" % index
+            if index in place:
+                return reuse.tile([P, GATHER], dtype, name=name, align_bytes=64, offset=place[index] * half_region)
+            return keep.tile([P, GATHER], dtype, name=name, align_bytes=64)
+
+        def gather(c):
+            entries = offs_t[:, c * GATHER // 16 : (c + 1) * GATHER // 16]
+            gw[c] = [gathered(4 * c + 2 * o, U32) for o in range(PASSES)]
+            gs[c] = [gathered(4 * c + 2 * o + 1, U8) for o in range(PASSES)]
+            for o in range(PASSES):
+                nc.vector.tensor_copy(gw[c][o][:], xw[o][:].indirect(entries))
+                nc.vector.tensor_copy(gs[c][o][:], xs[:, o, :].indirect(entries))
+
+        hq_shared = keep.tile([P, T], U32, name="hq_shared", align_bytes=64)
+        hs_shared = keep.tile([P, T], U8, name="hs_shared", align_bytes=64)
+        hq_routed = keep.tile([P, SLOTS], U32, name="hq_routed", align_bytes=64)
+        hs_routed = keep.tile([P, SLOTS], U8, name="hs_routed", align_bytes=64)
+
+        def first_layer(j, words, scales, e):
+            if e == SHARED:
+                planes = (s1_shared, s3_shared)
+                first = 0
+            else:
+                planes = (s1_routed, s3_routed)
+                first = e * PASSES
+            a = psum.tile([P, H], F32, name="a", tag="a")
+            b = psum.tile([P, H], F32, name="b", tag="b")
+            for acc, w, plane in ((a, w1[e], planes[0]), (b, w3[e], planes[1])):
+                for o in range(PASSES):
+                    nc.tensor.matmul_mx(
+                        out=acc[:],
+                        lhsT=words[o].bitcast(FP8X4),
+                        lhsT_scale=scales[o],
+                        rhs=w[:, o, :].bitcast(FP4X4),
+                        rhs_scale=plane[:, first + o, :],
+                        start=(o == 0),
+                        stop=(o == PASSES - 1),
+                    )
+            relu_a = reuse.tile([P, 2, P, 2], F32, name="relu_a%d" % j, align_bytes=64, offset=j * 4 * H)
+            nc.scalar.activation(relu_a[:], a[:].rearrange("p (m u d) -> p u m d", u=2, d=2), RELU)
+            h = ring.tile([P, 2, P, 2], BF16, name="h", bufs=4)
+            nc.vector.tensor_tensor(h[:], b[:].rearrange("p (m u d) -> p u m d", u=2, d=2), relu_a[:], MULT)
+            return h
+
+        def turn_and_quantize(hs, codes, scales):
+            count = len(hs)
+            turned = psum_t.tile([P, 2, 2, P], F32, name="turned")
+            for j, h in enumerate(hs):
+                pairs = h[:].rearrange("p u m d -> p u (m d)").bitcast(F32)
+                for u in range(2):
+                    nc.tensor.transpose(turned[:, j, u, :], pairs[:, u, :], ident[:])
+            grouped = ring.tile([P, 2, P, 2], F32, name="grouped", align_bytes=64)
+            nc.scalar.copy(grouped[:, 0:count, :, :], turned[:, 0:count, :, :].rearrange("p j u c -> p j c u"))
+            nc.vector.quantize_mx(
+                out=codes.bitcast(FP8X4),
+                scales=scales,
+                in_=grouped[:, 0:count, :, :].rearrange("p j c u -> p (j c u)").bitcast(BF16),
+            )
+
+        per_chunk = GATHER // C
+
+        def operands(j):
+            if j < T // P:
+                cols = slice(j * P, (j + 1) * P)
+                return [xw[o][:, cols] for o in range(PASSES)], [xs[:, o, cols] for o in range(PASSES)], SHARED
+            e = j - T // P
+            c = e // per_chunk
+            if e % per_chunk == 0:
+                gather(c)
+            cols = slice((e % per_chunk) * C, (e % per_chunk + 1) * C)
+            return [gw[c][o][:, cols] for o in range(PASSES)], [gs[c][o][:, cols] for o in range(PASSES)], e
+
+        def quantize_group(first, count):
+            if first < T // P:
+                codes, scales, col = hq_shared, hs_shared, first * P
+            else:
+                codes, scales, col = hq_routed, hs_routed, (first - T // P) * C
+            cols = slice(col, col + count * P)
+            turn_and_quantize(hidden[first : first + count], codes[:, cols], scales[:, cols])
+
+        hidden = []
+        after = {2: (0, 2), 4: (2, 2), 6: (4, 2), 8: (6, 2), 10: (8, 2), 11: (10, 1)}
+        for j in range(T // P + E):
+            hidden.append(first_layer(j, *operands(j)))
+            if j in after:
+                quantize_group(*after[j])
+
+        def second_layer(acc, e, codes, scales):
+            nc.tensor.matmul_mx(
+                out=acc,
+                lhsT=w2[:, e, :].bitcast(FP4X4),
+                lhsT_scale=s2[:, e, :],
+                rhs=codes.bitcast(FP8X4),
+                rhs_scale=scales,
+                start=True,
+                stop=True,
+            )
+
+        y = keep.tile([P, SLOTS], F32, name="y")
+
+        def routed_results(experts, tag):
+            acc = psum.tile([P, H], F32, name="y_acc", tag=tag)
+            for j, e in enumerate(experts):
+                cols = slice(e * C, (e + 1) * C)
+                second_layer(acc[:, j * C : (j + 1) * C], e, hq_routed[:, cols], hs_routed[:, cols])
+            nc.scalar.copy(y[:, experts[0] * C : (experts[-1] + 1) * C], acc[:, 0 : len(experts) * C])
+
+        routed_results([0, 1, 2, 3], "a")
+        routed_results([4, 5, 6], "a")
+        y_shared = psum.tile([P, T], F32, name="y_shared", tag="b")
+        second_layer(y_shared[:], SHARED, hq_shared[:], hs_shared[:])
+        quantize_group(11, 1)
+        routed_results([7], "b")
+
+        for half in range(2):
+            cols = slice(half * HALF, (half + 1) * HALF)
+            entries = slice(half * HALF // 16, (half + 1) * HALF // 16)
+            first = keep.tile([P, HALF], F32, name="first%d" % half)
+            second = keep.tile([P, HALF], F32, name="second%d" % half)
+            nc.vector.tensor_tensor(first[:], y[:].indirect(pos1_t[:, entries]), gate_t[:, 0, cols], MULT)
+            nc.vector.tensor_tensor(second[:], y[:].indirect(pos2_t[:, entries]), gate_t[:, 1, cols], MULT)
+            partial = keep.tile([P, HALF], F32, name="partial%d" % half)
+            nc.vector.tensor_tensor(partial[:], y_shared[:, cols], first[:], ADD)
+            total = keep.tile([P, HALF], F32, name="total%d" % half)
+            nc.vector.tensor_tensor(total[:], partial[:], second[:], ADD)
+            nc.sync.dma_start(out=out[:, cols], in_=total[:])

@@ -59,10 +59,8 @@ def tile_moe_shr_glu_relu_kernel(
         gate_t = keep.tile([P, 2, T], F32, name="gate_t")
         ident = keep.tile([P, P], F32, name="ident")
 
-        for plane in (xs, s1_shared, s3_shared, s3_routed):
+        for plane in (xs, s1_shared, s3_shared, s1_routed, s3_routed, s2):
             nc.vector.memset(plane[:].bitcast(I32), 0)
-        for plane in (s1_routed, s2):
-            nc.gpsimd.memset(plane[:].bitcast(I32), 0)
         make_identity(nc, ident[:])
 
         def load_words(tile, words):
@@ -73,15 +71,15 @@ def tile_moe_shr_glu_relu_kernel(
 
         nc.sync.dma_start(offs_t[:], offs)
         load_tokens(0)
-        load_words(w1[SHARED], w1_words[SHARED])
-        load_tokens(1)
-        load_words(w3[SHARED], w3_words[SHARED])
         load_plane(nc.sync, xs, x_scales)
+        load_words(w1[SHARED], w1_words[SHARED])
         load_plane(nc.sync, s1_shared, w1_scales[SHARED])
+        load_tokens(1)
         load_plane(nc.sync, s3_shared, w3_scales[SHARED])
-        load_plane(nc.sync, s1_routed, w1_scales[0:E].rearrange("e s f c -> (e s) f c"))
-        load_plane(nc.sync, s3_routed, w3_scales[0:E].rearrange("e s f c -> (e s) f c"))
-        load_plane(nc.sync, s2, w2_scales.rearrange("e s f c -> (e s) f c"))
+        load_words(w3[SHARED], w3_words[SHARED])
+        load_plane(nc.gpsimd, s1_routed, w1_scales[0:E].rearrange("e s f c -> (e s) f c"))
+        load_plane(nc.gpsimd, s3_routed, w3_scales[0:E].rearrange("e s f c -> (e s) f c"))
+        load_plane(nc.gpsimd, s2, w2_scales.rearrange("e s f c -> (e s) f c"))
         for e in range(E):
             load_words(w1[e], w1_words[e])
             load_words(w3[e], w3_words[e])
@@ -210,15 +208,15 @@ def tile_moe_shr_glu_relu_kernel(
         quantize_group(11, 1)
         routed_results([7], "b")
 
-        for half in range(2):
-            cols = slice(half * HALF, (half + 1) * HALF)
-            entries = slice(half * HALF // 16, (half + 1) * HALF // 16)
-            first = keep.tile([P, HALF], F32, name="first%d" % half)
-            second = keep.tile([P, HALF], F32, name="second%d" % half)
-            nc.vector.tensor_tensor(first[:], y[:].indirect(pos1_t[:, entries]), gate_t[:, 0, cols], MULT)
-            nc.vector.tensor_tensor(second[:], y[:].indirect(pos2_t[:, entries]), gate_t[:, 1, cols], MULT)
-            partial = keep.tile([P, HALF], F32, name="partial%d" % half)
-            nc.vector.tensor_tensor(partial[:], y_shared[:, cols], first[:], ADD)
-            total = keep.tile([P, HALF], F32, name="total%d" % half)
-            nc.vector.tensor_tensor(total[:], partial[:], second[:], ADD)
-            nc.sync.dma_start(out=out[:, cols], in_=total[:])
+        first = keep.tile([P, T], F32, name="first")
+        second = keep.tile([P, T], F32, name="second")
+        nc.vector.tensor_tensor(first[:], y[:].indirect(pos1_t[:]), gate_t[:, 0, :], MULT)
+        nc.vector.tensor_tensor(second[:], y[:].indirect(pos2_t[:]), gate_t[:, 1, :], MULT)
+        halves = [slice(half * HALF, (half + 1) * HALF) for half in range(2)]
+        partial = keep.tile([P, T], F32, name="partial")
+        total = keep.tile([P, T], F32, name="total")
+        for cols in halves:
+            nc.vector.tensor_tensor(partial[:, cols], y_shared[:, cols], first[:, cols], ADD)
+        for cols in halves:
+            nc.vector.tensor_tensor(total[:, cols], partial[:, cols], second[:, cols], ADD)
+            nc.sync.dma_start(out=out[:, cols], in_=total[:, cols])

@@ -24,6 +24,10 @@ SLOTS = E * C
 SHARED = E
 GATHER = 256
 HALF = T // 2
+GROUPS = (range(4, E + 1), range(0, 4))
+ORDER = (4, 5, 6, 7, 0, 1, 2, 3)
+EARLY = 3
+LAST = T // P + E - 1
 
 
 def load_plane(queue, plane, rows):
@@ -40,47 +44,57 @@ def tile_moe_shr_glu_relu_kernel(
         keep = ctx.enter_context(tc.tile_pool(name="keep", bufs=1))
         ring = ctx.enter_context(tc.tile_pool(name="ring", bufs=3))
         reuse = ctx.enter_context(tc.tile_pool(name="reuse", bufs=1))
-        psum = ctx.enter_context(tc.psum_pool(name="psum", bufs=3))
-        psum_t = ctx.enter_context(tc.psum_pool(name="psum_t", bufs=2))
+        psum = ctx.enter_context(tc.psum_pool(name="psum", bufs=1))
 
         offs_t = keep.tile([P, SLOTS // 16], U16, name="offs_t")
         pos1_t = keep.tile([P, T // 16], U16, name="pos1_t")
         pos2_t = keep.tile([P, T // 16], U16, name="pos2_t")
-        xw = [keep.tile([P, T], U32, name="xw%d" % o, align_bytes=64) for o in range(PASSES)]
-        xs = keep.tile([P, PASSES, T], U8, name="xs", align_bytes=64)
+        xw = keep.tile([P, PASSES, T], U32, name="xw", align_bytes=64)
+        xs = keep.tile([P, T], U8, name="xs", align_bytes=64)
+        xs_second = keep.tile([P, 1, T], U8, name="xs_second", align_bytes=64)
+        gs = keep.tile([P, SLOTS], U8, name="gs", align_bytes=64)
+        gs_second = keep.tile([P, SLOTS], U8, name="gs_second", align_bytes=64)
         w1 = [keep.tile([P, PASSES, 2 * H], U8, name="w1_%d" % e, align_bytes=64) for e in range(E + 1)]
         w3 = [keep.tile([P, PASSES, 2 * H], U8, name="w3_%d" % e, align_bytes=64) for e in range(E + 1)]
         w2 = keep.tile([P, E + 1, 2 * N], U8, name="w2", align_bytes=64)
-        s1_shared = keep.tile([P, PASSES, H], U8, name="s1_shared", align_bytes=64)
-        s3_shared = keep.tile([P, PASSES, H], U8, name="s3_shared", align_bytes=64)
-        s1_routed = keep.tile([P, E * PASSES, H], U8, name="s1_routed", align_bytes=64)
-        s3_routed = keep.tile([P, E * PASSES, H], U8, name="s3_routed", align_bytes=64)
+        s1 = [keep.tile([P, len(group) * PASSES, H], U8, name="s1_%d" % g, align_bytes=64) for g, group in enumerate(GROUPS)]
+        s3 = [keep.tile([P, len(group) * PASSES, H], U8, name="s3_%d" % g, align_bytes=64) for g, group in enumerate(GROUPS)]
         s2 = keep.tile([P, E + 1, N], U8, name="s2", align_bytes=64)
         gate_t = keep.tile([P, 2, T], F32, name="gate_t")
         ident = keep.tile([P, P], F32, name="ident")
 
-        for plane in (xs, s1_shared, s3_shared, s1_routed, s3_routed, s2):
+        for plane in (xs, s1[0], xs_second, s3[0], gs_second, s1[1], s3[1], s2):
             nc.vector.memset(plane[:].bitcast(I32), 0)
         make_identity(nc, ident[:])
 
         def load_words(tile, words):
             nc.sync.dma_start(out=tile[:].bitcast(I32), in_=words.rearrange("s p c -> p s c").bitcast(I32))
 
-        def load_tokens(o):
-            nc.sync.dma_start(out=xw[o][:].bitcast(I32), in_=x_words[o].rearrange("p t r -> p (t r)").bitcast(I32))
+        def load_group_plane(plane, scales, g):
+            experts = slice(GROUPS[g].start, GROUPS[g].stop)
+            load_plane(nc.sync, plane[g], scales[experts].rearrange("e s f c -> (e s) f c"))
 
         nc.sync.dma_start(offs_t[:], offs)
-        load_tokens(0)
-        load_plane(nc.sync, xs, x_scales)
+        nc.sync.dma_start(out=xw[:].bitcast(I32), in_=x_words.rearrange("o p t r -> p o (t r)").bitcast(I32))
+        for q in range(4):
+            nc.sync.dma_start(out=xs[32 * q : 32 * q + 8, :].bitcast(I32), in_=x_scales[:, 4 * q : 4 * q + 4, :].bitcast(I32))
         load_words(w1[SHARED], w1_words[SHARED])
-        load_plane(nc.sync, s1_shared, w1_scales[SHARED])
-        load_tokens(1)
-        load_plane(nc.sync, s3_shared, w3_scales[SHARED])
+        load_group_plane(s1, w1_scales, 0)
+        load_plane(nc.sync, xs_second, x_scales[1:2])
+        load_group_plane(s3, w3_scales, 0)
         load_words(w3[SHARED], w3_words[SHARED])
-        load_plane(nc.gpsimd, s1_routed, w1_scales[0:E].rearrange("e s f c -> (e s) f c"))
-        load_plane(nc.gpsimd, s3_routed, w3_scales[0:E].rearrange("e s f c -> (e s) f c"))
-        load_plane(nc.gpsimd, s2, w2_scales.rearrange("e s f c -> (e s) f c"))
-        for e in range(E):
+        for first, count in ((0, 384), (384, 384), (768, 256)):
+            nc.vector.tensor_copy(gs[:, first : first + count], xs[:].indirect(offs_t[:, first // 16 : (first + count) // 16]))
+        for i, e in enumerate(ORDER):
+            if i == 1:
+                for first, count in ((0, 64), (64, 32), (96, 16)):
+                    nc.sync.dma_start(
+                        out=gs_second[first : first + count, :].bitcast(I32), in_=gs[first + 4 : first + 4 + count, :].bitcast(I32)
+                    )
+            if i == 2:
+                load_group_plane(s1, w1_scales, 1)
+                load_group_plane(s3, w3_scales, 1)
+                load_plane(nc.sync, s2, w2_scales.rearrange("e s f c -> (e s) f c"))
             load_words(w1[e], w1_words[e])
             load_words(w3[e], w3_words[e])
         load_words(w2, w2_words.rearrange("e s p c -> (e s) p c"))
@@ -89,38 +103,29 @@ def tile_moe_shr_glu_relu_kernel(
         nc.sync.dma_start(out=gate_t[:], in_=gate.rearrange("r p t -> p r t"))
 
         gw = {}
-        gs = {}
-        half_region = 2 * H
-        place = {7: 0, 8: 1, 9: 2, 10: 4, 11: 6, 12: 8, 13: 10, 14: 12, 15: 14}
-
-        def gathered(index, dtype):
-            name = "gathered%d" % index
-            if index in place:
-                return reuse.tile([P, GATHER], dtype, name=name, align_bytes=64, offset=place[index] * half_region)
-            return keep.tile([P, GATHER], dtype, name=name, align_bytes=64)
+        region = {(0, 1): 0, (1, 0): 1, (1, 1): 2}
 
         def gather(c):
             entries = offs_t[:, c * GATHER // 16 : (c + 1) * GATHER // 16]
-            gw[c] = [gathered(4 * c + 2 * o, U32) for o in range(PASSES)]
-            gs[c] = [gathered(4 * c + 2 * o + 1, U8) for o in range(PASSES)]
+            gw[c] = []
             for o in range(PASSES):
-                nc.vector.tensor_copy(gw[c][o][:], xw[o][:].indirect(entries))
-                nc.vector.tensor_copy(gs[c][o][:], xs[:, o, :].indirect(entries))
+                name = "gw%d_%d" % (c, o)
+                if (c, o) in region:
+                    words = reuse.tile([P, GATHER], U32, name=name, align_bytes=64, offset=region[(c, o)] * 4 * H)
+                else:
+                    words = keep.tile([P, GATHER], U32, name=name, align_bytes=64)
+                nc.vector.tensor_copy(words[:], xw[:, o, :].indirect(entries))
+                gw[c].append(words)
 
-        hq_shared = keep.tile([P, T], U32, name="hq_shared", align_bytes=64)
-        hs_shared = keep.tile([P, T], U8, name="hs_shared", align_bytes=64)
-        hq_routed = keep.tile([P, SLOTS], U32, name="hq_routed", align_bytes=64)
-        hs_routed = keep.tile([P, SLOTS], U8, name="hs_routed", align_bytes=64)
+        hq = keep.tile([P, T + SLOTS], U32, name="hq", align_bytes=64)
+        hs = keep.tile([P, T + SLOTS], U8, name="hs", align_bytes=64)
 
         def first_layer(j, words, scales, e):
-            if e == SHARED:
-                planes = (s1_shared, s3_shared)
-                first = 0
-            else:
-                planes = (s1_routed, s3_routed)
-                first = e * PASSES
-            a = psum.tile([P, H], F32, name="a", tag="a")
-            b = psum.tile([P, H], F32, name="b", tag="b")
+            g = 0 if e in GROUPS[0] else 1
+            planes = (s1[g], s3[g])
+            first = (e - GROUPS[g].start) * PASSES
+            a = psum.tile([P, H], F32, name="a", tag="a%d" % (min(j, LAST - 1) % 5))
+            b = psum.tile([P, H], F32, name="b", tag="b%d" % (j % 3))
             for acc, w, plane in ((a, w1[e], planes[0]), (b, w3[e], planes[1])):
                 for o in range(PASSES):
                     nc.tensor.matmul_mx(
@@ -138,10 +143,10 @@ def tile_moe_shr_glu_relu_kernel(
             nc.vector.tensor_tensor(h[:], b[:].rearrange("p (m u d) -> p u m d", u=2, d=2), relu_a[:], MULT)
             return h
 
-        def turn_and_quantize(hs, codes, scales):
-            count = len(hs)
-            turned = psum_t.tile([P, 2, 2, P], F32, name="turned")
-            for j, h in enumerate(hs):
+        def turn_and_quantize(tiles, codes, scales, bank):
+            count = len(tiles)
+            turned = psum.tile([P, 2, 2, P], F32, name="turned", tag=bank)
+            for j, h in enumerate(tiles):
                 pairs = h[:].rearrange("p u m d -> p u (m d)").bitcast(F32)
                 for u in range(2):
                     nc.tensor.transpose(turned[:, j, u, :], pairs[:, u, :], ident[:])
@@ -156,30 +161,30 @@ def tile_moe_shr_glu_relu_kernel(
         per_chunk = GATHER // C
 
         def operands(j):
-            if j < T // P:
-                cols = slice(j * P, (j + 1) * P)
-                return [xw[o][:, cols] for o in range(PASSES)], [xs[:, o, cols] for o in range(PASSES)], SHARED
-            e = j - T // P
+            if j < EARLY or j == LAST:
+                first = min(j, EARLY) * P
+                cols = slice(first, first + P)
+                return [xw[:, o, cols] for o in range(PASSES)], [xs[:, cols], xs_second[:, 0, cols]], SHARED
+            e = ORDER[j - EARLY]
             c = e // per_chunk
             if e % per_chunk == 0:
                 gather(c)
             cols = slice((e % per_chunk) * C, (e % per_chunk + 1) * C)
-            return [gw[c][o][:, cols] for o in range(PASSES)], [gs[c][o][:, cols] for o in range(PASSES)], e
+            slots = slice(e * C, (e + 1) * C)
+            return [gw[c][o][:, cols] for o in range(PASSES)], [gs[:, slots], gs_second[:, slots]], e
 
-        def quantize_group(first, count):
-            if first < T // P:
-                codes, scales, col = hq_shared, hs_shared, first * P
-            else:
-                codes, scales, col = hq_routed, hs_routed, (first - T // P) * C
-            cols = slice(col, col + count * P)
-            turn_and_quantize(hidden[first : first + count], codes[:, cols], scales[:, cols])
+        def quantize_group(first, count, bank):
+            cols = slice(first * P, (first + count) * P)
+            turn_and_quantize(hidden[first : first + count], hq[:, cols], hs[:, cols], bank)
 
         hidden = []
-        after = {2: (0, 2), 4: (2, 2), 6: (4, 2), 8: (6, 2), 10: (8, 2), 11: (10, 1)}
-        for j in range(T // P + E):
+        for j in range(LAST):
             hidden.append(first_layer(j, *operands(j)))
-            if j in after:
-                quantize_group(*after[j])
+            if j in (1, LAST - 1):
+                quantize_group(j - 1, 1, "a%d" % (j % 5))
+            elif j % 2 == 1:
+                quantize_group(j - 2, 2, "a%d" % (j % 5))
+        quantize_group(LAST - 1, 1, "a1")
 
         def second_layer(acc, e, codes, scales):
             nc.tensor.matmul_mx(
@@ -194,19 +199,23 @@ def tile_moe_shr_glu_relu_kernel(
 
         y = keep.tile([P, SLOTS], F32, name="y")
 
-        def routed_results(experts, tag):
+        def routed_results(experts, tag, copy):
             acc = psum.tile([P, H], F32, name="y_acc", tag=tag)
-            for j, e in enumerate(experts):
-                cols = slice(e * C, (e + 1) * C)
-                second_layer(acc[:, j * C : (j + 1) * C], e, hq_routed[:, cols], hs_routed[:, cols])
-            nc.scalar.copy(y[:, experts[0] * C : (experts[-1] + 1) * C], acc[:, 0 : len(experts) * C])
+            for i, e in enumerate(experts):
+                j = EARLY + ORDER.index(e)
+                cols = slice(j * P, (j + 1) * P)
+                second_layer(acc[:, i * C : (i + 1) * C], e, hq[:, cols], hs[:, cols])
+            copy(y[:, experts[0] * C : (experts[-1] + 1) * C], acc[:, 0 : len(experts) * C])
 
-        routed_results([0, 1, 2, 3], "a")
-        routed_results([4, 5, 6], "a")
-        y_shared = psum.tile([P, T], F32, name="y_shared", tag="b")
-        second_layer(y_shared[:], SHARED, hq_shared[:], hs_shared[:])
-        quantize_group(11, 1)
-        routed_results([7], "b")
+        routed_results([2, 3], "b0", nc.scalar.copy)
+        routed_results([4, 5, 6, 7], "a3", nc.vector.tensor_copy)
+        routed_results([0, 1], "a4", nc.scalar.copy)
+        hidden.append(first_layer(LAST, *operands(LAST)))
+        quantize_group(LAST, 1, "a2")
+        y_shared = psum.tile([P, T], F32, name="y_shared", tag="b1")
+        for first_token, first_col, width in ((0, 0, 2 * P), (2 * P, 2 * P, P), (EARLY * P, LAST * P, P)):
+            cols = slice(first_col, first_col + width)
+            second_layer(y_shared[:, first_token : first_token + width], SHARED, hq[:, cols], hs[:, cols])
 
         first = keep.tile([P, T], F32, name="first")
         second = keep.tile([P, T], F32, name="second")

@@ -24,10 +24,9 @@ SLOTS = E * C
 SHARED = E
 GATHER = 256
 HALF = T // 2
-GROUPS = (range(4, E + 1), range(0, 4))
-ORDER = (4, 5, 6, 7, 0, 1, 2, 3)
-EARLY = 3
-LAST = T // P + E - 1
+GROUPS = (range(E, E + 1), range(0, 3), range(3, 6), range(6, 8))
+JOBS = [("s", 0), ("s", 1), ("s", 2), ("e", 0), ("e", 1), ("e", 2), ("s", 3), ("e", 3), ("e", 4), ("e", 5), ("e", 6), ("e", 7)]
+A_BANK = ["a0", "a1", "a2", "a3", "a4", "a0", "a0", "a1", "a2", "a3", "a4", "a1"]
 
 
 def load_plane(queue, plane, rows):
@@ -43,17 +42,14 @@ def tile_moe_shr_glu_relu_kernel(
     with ExitStack() as ctx:
         keep = ctx.enter_context(tc.tile_pool(name="keep", bufs=1))
         ring = ctx.enter_context(tc.tile_pool(name="ring", bufs=3))
-        reuse = ctx.enter_context(tc.tile_pool(name="reuse", bufs=1))
+        chunks = ctx.enter_context(tc.tile_pool(name="chunks", bufs=2))
         psum = ctx.enter_context(tc.psum_pool(name="psum", bufs=1))
 
         offs_t = keep.tile([P, SLOTS // 16], U16, name="offs_t")
         pos1_t = keep.tile([P, T // 16], U16, name="pos1_t")
         pos2_t = keep.tile([P, T // 16], U16, name="pos2_t")
         xw = keep.tile([P, PASSES, T], U32, name="xw", align_bytes=64)
-        xs = keep.tile([P, T], U8, name="xs", align_bytes=64)
-        xs_second = keep.tile([P, 1, T], U8, name="xs_second", align_bytes=64)
-        gs = keep.tile([P, SLOTS], U8, name="gs", align_bytes=64)
-        gs_second = keep.tile([P, SLOTS], U8, name="gs_second", align_bytes=64)
+        xs = keep.tile([P, PASSES, T], U8, name="xs", align_bytes=64)
         w1 = [keep.tile([P, PASSES, 2 * H], U8, name="w1_%d" % e, align_bytes=64) for e in range(E + 1)]
         w3 = [keep.tile([P, PASSES, 2 * H], U8, name="w3_%d" % e, align_bytes=64) for e in range(E + 1)]
         w2 = keep.tile([P, E + 1, 2 * N], U8, name="w2", align_bytes=64)
@@ -63,7 +59,7 @@ def tile_moe_shr_glu_relu_kernel(
         gate_t = keep.tile([P, 2, T], F32, name="gate_t")
         ident = keep.tile([P, P], F32, name="ident")
 
-        for plane in (xs, s1[0], xs_second, s3[0], gs_second, s1[1], s3[1], s2):
+        for plane in (xs, s1[0], s3[0], s1[1], s3[1], s1[2], s3[2], s2, s1[3], s3[3]):
             nc.vector.memset(plane[:].bitcast(I32), 0)
         make_identity(nc, ident[:])
 
@@ -76,55 +72,47 @@ def tile_moe_shr_glu_relu_kernel(
 
         nc.sync.dma_start(offs_t[:], offs)
         nc.sync.dma_start(out=xw[:].bitcast(I32), in_=x_words.rearrange("o p t r -> p o (t r)").bitcast(I32))
-        for q in range(4):
-            nc.sync.dma_start(out=xs[32 * q : 32 * q + 8, :].bitcast(I32), in_=x_scales[:, 4 * q : 4 * q + 4, :].bitcast(I32))
+        load_plane(nc.sync, xs, x_scales)
         load_words(w1[SHARED], w1_words[SHARED])
         load_group_plane(s1, w1_scales, 0)
-        load_plane(nc.sync, xs_second, x_scales[1:2])
-        load_group_plane(s3, w3_scales, 0)
         load_words(w3[SHARED], w3_words[SHARED])
-        for first, count in ((0, 384), (384, 384), (768, 256)):
-            nc.vector.tensor_copy(gs[:, first : first + count], xs[:].indirect(offs_t[:, first // 16 : (first + count) // 16]))
-        for i, e in enumerate(ORDER):
-            if i == 1:
-                for first, count in ((0, 64), (64, 32), (96, 16)):
-                    nc.sync.dma_start(
-                        out=gs_second[first : first + count, :].bitcast(I32), in_=gs[first + 4 : first + 4 + count, :].bitcast(I32)
-                    )
-            if i == 2:
-                load_group_plane(s1, w1_scales, 1)
-                load_group_plane(s3, w3_scales, 1)
+        load_group_plane(s3, w3_scales, 0)
+        for g in range(1, len(GROUPS)):
+            load_group_plane(s1, w1_scales, g)
+            load_group_plane(s3, w3_scales, g)
+            if g == 2:
                 load_plane(nc.sync, s2, w2_scales.rearrange("e s f c -> (e s) f c"))
-            load_words(w1[e], w1_words[e])
-            load_words(w3[e], w3_words[e])
+            for e in GROUPS[g]:
+                load_words(w1[e], w1_words[e])
+                load_words(w3[e], w3_words[e])
         load_words(w2, w2_words.rearrange("e s p c -> (e s) p c"))
         nc.sync.dma_start(pos1_t[:], pos1)
         nc.sync.dma_start(pos2_t[:], pos2)
         nc.sync.dma_start(out=gate_t[:], in_=gate.rearrange("r p t -> p r t"))
 
         gw = {}
-        region = {(0, 1): 0, (1, 0): 1, (1, 1): 2}
+        gs = {}
 
         def gather(c):
             entries = offs_t[:, c * GATHER // 16 : (c + 1) * GATHER // 16]
             gw[c] = []
+            gs[c] = []
             for o in range(PASSES):
-                name = "gw%d_%d" % (c, o)
-                if (c, o) in region:
-                    words = reuse.tile([P, GATHER], U32, name=name, align_bytes=64, offset=region[(c, o)] * 4 * H)
-                else:
-                    words = keep.tile([P, GATHER], U32, name=name, align_bytes=64)
+                words = chunks.tile([P, GATHER], U32, name="gw%d" % o, align_bytes=64)
                 nc.vector.tensor_copy(words[:], xw[:, o, :].indirect(entries))
                 gw[c].append(words)
+                scales = chunks.tile([P, GATHER], U8, name="gs%d" % o, align_bytes=64)
+                nc.vector.tensor_copy(scales[:], xs[:, o, :].indirect(entries))
+                gs[c].append(scales)
 
         hq = keep.tile([P, T + SLOTS], U32, name="hq", align_bytes=64)
         hs = keep.tile([P, T + SLOTS], U8, name="hs", align_bytes=64)
 
         def first_layer(j, words, scales, e):
-            g = 0 if e in GROUPS[0] else 1
+            g = [e in group for group in GROUPS].index(True)
             planes = (s1[g], s3[g])
             first = (e - GROUPS[g].start) * PASSES
-            a = psum.tile([P, H], F32, name="a", tag="a%d" % (min(j, LAST - 1) % 5))
+            a = psum.tile([P, H], F32, name="a", tag=A_BANK[j])
             b = psum.tile([P, H], F32, name="b", tag="b%d" % (j % 3))
             for acc, w, plane in ((a, w1[e], planes[0]), (b, w3[e], planes[1])):
                 for o in range(PASSES):
@@ -137,7 +125,7 @@ def tile_moe_shr_glu_relu_kernel(
                         start=(o == 0),
                         stop=(o == PASSES - 1),
                     )
-            relu_a = reuse.tile([P, 2, P, 2], F32, name="relu_a%d" % j, align_bytes=64, offset=j * 4 * H)
+            relu_a = ring.tile([P, 2, P, 2], F32, name="relu_a", align_bytes=64)
             nc.scalar.activation(relu_a[:], a[:].rearrange("p (m u d) -> p u m d", u=2, d=2), RELU)
             h = ring.tile([P, 2, P, 2], BF16, name="h", bufs=4)
             nc.vector.tensor_tensor(h[:], b[:].rearrange("p (m u d) -> p u m d", u=2, d=2), relu_a[:], MULT)
@@ -161,30 +149,29 @@ def tile_moe_shr_glu_relu_kernel(
         per_chunk = GATHER // C
 
         def operands(j):
-            if j < EARLY or j == LAST:
-                first = min(j, EARLY) * P
-                cols = slice(first, first + P)
-                return [xw[:, o, cols] for o in range(PASSES)], [xs[:, cols], xs_second[:, 0, cols]], SHARED
-            e = ORDER[j - EARLY]
-            c = e // per_chunk
-            if e % per_chunk == 0:
+            kind, n = JOBS[j]
+            if kind == "s":
+                cols = slice(n * P, (n + 1) * P)
+                return [xw[:, o, cols] for o in range(PASSES)], [xs[:, o, cols] for o in range(PASSES)], SHARED
+            c = n // per_chunk
+            if n % per_chunk == 0:
                 gather(c)
-            cols = slice((e % per_chunk) * C, (e % per_chunk + 1) * C)
-            slots = slice(e * C, (e + 1) * C)
-            return [gw[c][o][:, cols] for o in range(PASSES)], [gs[:, slots], gs_second[:, slots]], e
+            cols = slice((n % per_chunk) * C, (n % per_chunk + 1) * C)
+            return [gw[c][o][:, cols] for o in range(PASSES)], [gs[c][o][:, cols] for o in range(PASSES)], n
 
         def quantize_group(first, count, bank):
             cols = slice(first * P, (first + count) * P)
             turn_and_quantize(hidden[first : first + count], hq[:, cols], hs[:, cols], bank)
 
         hidden = []
-        for j in range(LAST):
+        last = len(JOBS) - 1
+        for j in range(len(JOBS)):
             hidden.append(first_layer(j, *operands(j)))
-            if j in (1, LAST - 1):
-                quantize_group(j - 1, 1, "a%d" % (j % 5))
-            elif j % 2 == 1:
-                quantize_group(j - 2, 2, "a%d" % (j % 5))
-        quantize_group(LAST - 1, 1, "a1")
+            if j == last:
+                quantize_group(j - 1, 1, A_BANK[j])
+            elif j % 2 == 0 and j > 0:
+                quantize_group(j - 2, 2, A_BANK[j])
+        quantize_group(last, 1, "b1")
 
         def second_layer(acc, e, codes, scales):
             nc.tensor.matmul_mx(
@@ -202,18 +189,16 @@ def tile_moe_shr_glu_relu_kernel(
         def routed_results(experts, tag, copy):
             acc = psum.tile([P, H], F32, name="y_acc", tag=tag)
             for i, e in enumerate(experts):
-                j = EARLY + ORDER.index(e)
+                j = JOBS.index(("e", e))
                 cols = slice(j * P, (j + 1) * P)
                 second_layer(acc[:, i * C : (i + 1) * C], e, hq[:, cols], hs[:, cols])
             copy(y[:, experts[0] * C : (experts[-1] + 1) * C], acc[:, 0 : len(experts) * C])
 
-        routed_results([2, 3], "b0", nc.scalar.copy)
-        routed_results([4, 5, 6, 7], "a3", nc.vector.tensor_copy)
-        routed_results([0, 1], "a4", nc.scalar.copy)
-        hidden.append(first_layer(LAST, *operands(LAST)))
-        quantize_group(LAST, 1, "a2")
-        y_shared = psum.tile([P, T], F32, name="y_shared", tag="b1")
-        for first_token, first_col, width in ((0, 0, 2 * P), (2 * P, 2 * P, P), (EARLY * P, LAST * P, P)):
+        routed_results([7], "b0", nc.vector.tensor_copy)
+        routed_results([0, 1, 2, 3], "a2", nc.scalar.copy)
+        routed_results([4, 5, 6], "a3", nc.scalar.copy)
+        y_shared = psum.tile([P, T], F32, name="y_shared", tag="a0")
+        for first_token, first_col, width in ((0, 0, 2 * P), (2 * P, 2 * P, P), (3 * P, JOBS.index(("s", 3)) * P, P)):
             cols = slice(first_col, first_col + width)
             second_layer(y_shared[:, first_token : first_token + width], SHARED, hq[:, cols], hs[:, cols])
 

@@ -24,9 +24,10 @@ SLOTS = E * C
 SHARED = E
 GATHER = 256
 HALF = T // 2
-GROUPS = (range(E, E + 1), range(0, 3), range(3, 6), range(6, 8))
-JOBS = [("s", 0), ("s", 1), ("s", 2), ("e", 0), ("e", 1), ("e", 2), ("s", 3), ("e", 3), ("e", 4), ("e", 5), ("e", 6), ("e", 7)]
-A_BANK = ["a0", "a1", "a2", "a3", "a4", "a0", "a0", "a1", "a2", "a3", "a4", "a1"]
+GROUPS = (range(6, E + 1), range(0, 6))
+ORDER = (7, 6, 5, 4, 3, 2, 1, 0)
+QUARTERS = T // P
+LATE = {(1, 1, "s"): (2, 0), (1, 1, "w"): (3, 0), (0, 0, "w"): (3, 1024), (0, 0, "s"): (5, 0), (0, 1, "w"): (5, 1024), (0, 1, "s"): (7, 0)}
 
 
 def load_plane(queue, plane, rows):
@@ -42,7 +43,7 @@ def tile_moe_shr_glu_relu_kernel(
     with ExitStack() as ctx:
         keep = ctx.enter_context(tc.tile_pool(name="keep", bufs=1))
         ring = ctx.enter_context(tc.tile_pool(name="ring", bufs=3))
-        chunks = ctx.enter_context(tc.tile_pool(name="chunks", bufs=2))
+        reuse = ctx.enter_context(tc.tile_pool(name="reuse", bufs=1))
         psum = ctx.enter_context(tc.psum_pool(name="psum", bufs=1))
 
         offs_t = keep.tile([P, SLOTS // 16], U16, name="offs_t")
@@ -50,7 +51,8 @@ def tile_moe_shr_glu_relu_kernel(
         pos2_t = keep.tile([P, T // 16], U16, name="pos2_t")
         xw = keep.tile([P, PASSES, T], U32, name="xw", align_bytes=64)
         xs = keep.tile([P, PASSES, T], U8, name="xs", align_bytes=64)
-        w1 = [keep.tile([P, PASSES, 2 * H], U8, name="w1_%d" % e, align_bytes=64) for e in range(E + 1)]
+        w1 = [keep.tile([P, 2 * PASSES, 2 * H], U8, name="w1_%d" % c, align_bytes=64) for c in range(E // 2)]
+        w1_shared = keep.tile([P, PASSES, 2 * H], U8, name="w1_shared", align_bytes=64)
         w3 = [keep.tile([P, PASSES, 2 * H], U8, name="w3_%d" % e, align_bytes=64) for e in range(E + 1)]
         w2 = keep.tile([P, E + 1, 2 * N], U8, name="w2", align_bytes=64)
         s1 = [keep.tile([P, len(group) * PASSES, H], U8, name="s1_%d" % g, align_bytes=64) for g, group in enumerate(GROUPS)]
@@ -59,33 +61,33 @@ def tile_moe_shr_glu_relu_kernel(
         gate_t = keep.tile([P, 2, T], F32, name="gate_t")
         ident = keep.tile([P, P], F32, name="ident")
 
-        for plane in (xs, s1[0], s3[0], s1[1], s3[1], s1[2], s3[2], s2, s1[3], s3[3]):
+        for plane in (xs, s1[0], s3[0], s1[1], s3[1], s2):
             nc.vector.memset(plane[:].bitcast(I32), 0)
         make_identity(nc, ident[:])
 
         def load_words(tile, words):
             nc.sync.dma_start(out=tile[:].bitcast(I32), in_=words.rearrange("s p c -> p s c").bitcast(I32))
 
-        def load_group_plane(plane, scales, g):
+        def load_group_plane(queue, plane, scales, g):
             experts = slice(GROUPS[g].start, GROUPS[g].stop)
-            load_plane(nc.sync, plane[g], scales[experts].rearrange("e s f c -> (e s) f c"))
+            load_plane(queue, plane[g], scales[experts].rearrange("e s f c -> (e s) f c"))
 
         nc.sync.dma_start(offs_t[:], offs)
         nc.sync.dma_start(out=xw[:].bitcast(I32), in_=x_words.rearrange("o p t r -> p o (t r)").bitcast(I32))
         load_plane(nc.sync, xs, x_scales)
-        load_words(w1[SHARED], w1_words[SHARED])
-        load_group_plane(s1, w1_scales, 0)
+        load_words(w1_shared, w1_words[SHARED])
+        load_group_plane(nc.sync, s1, w1_scales, 0)
         load_words(w3[SHARED], w3_words[SHARED])
-        load_group_plane(s3, w3_scales, 0)
-        for g in range(1, len(GROUPS)):
-            load_group_plane(s1, w1_scales, g)
-            load_group_plane(s3, w3_scales, g)
-            if g == 2:
-                load_plane(nc.sync, s2, w2_scales.rearrange("e s f c -> (e s) f c"))
-            for e in GROUPS[g]:
-                load_words(w1[e], w1_words[e])
-                load_words(w3[e], w3_words[e])
+        load_group_plane(nc.sync, s3, w3_scales, 0)
+        load_group_plane(nc.gpsimd, s1, w1_scales, 1)
+        load_group_plane(nc.gpsimd, s3, w3_scales, 1)
+        for i, e in enumerate(ORDER):
+            if i % 2 == 0:
+                c = e // 2
+                load_words(w1[c], w1_words[2 * c : 2 * c + 2].rearrange("e s p c -> (e s) p c"))
+            load_words(w3[e], w3_words[e])
         load_words(w2, w2_words.rearrange("e s p c -> (e s) p c"))
+        load_plane(nc.sync, s2, w2_scales.rearrange("e s f c -> (e s) f c"))
         nc.sync.dma_start(pos1_t[:], pos1)
         nc.sync.dma_start(pos2_t[:], pos2)
         nc.sync.dma_start(out=gate_t[:], in_=gate.rearrange("r p t -> p r t"))
@@ -93,43 +95,74 @@ def tile_moe_shr_glu_relu_kernel(
         gw = {}
         gs = {}
 
-        def gather(c):
+        def gathered_tile(c, o, sort, dtype):
+            name = "g%s%d_%d" % (sort, c, o)
+            if (c, o, sort) in LATE:
+                j, offset = LATE[(c, o, sort)]
+                return reuse.tile([P, GATHER], dtype, name=name, align_bytes=64, offset=j * 4 * H + offset)
+            return keep.tile([P, GATHER], dtype, name=name, align_bytes=64)
+
+        def gather(c, o, sort):
             entries = offs_t[:, c * GATHER // 16 : (c + 1) * GATHER // 16]
-            gw[c] = []
-            gs[c] = []
+            if sort == "w":
+                gw[(c, o)] = gathered_tile(c, o, sort, U32)
+                nc.vector.tensor_copy(gw[(c, o)][:], xw[:, o, :].indirect(entries))
+            else:
+                gs[(c, o)] = gathered_tile(c, o, sort, U8)
+                nc.vector.tensor_copy(gs[(c, o)][:], xs[:, o, :].indirect(entries))
+
+        for c in (3, 2, 1, 0):
             for o in range(PASSES):
-                words = chunks.tile([P, GATHER], U32, name="gw%d" % o, align_bytes=64)
-                nc.vector.tensor_copy(words[:], xw[:, o, :].indirect(entries))
-                gw[c].append(words)
-                scales = chunks.tile([P, GATHER], U8, name="gs%d" % o, align_bytes=64)
-                nc.vector.tensor_copy(scales[:], xs[:, o, :].indirect(entries))
-                gs[c].append(scales)
+                for sort in ("w", "s"):
+                    if (c, o, sort) not in LATE:
+                        gather(c, o, sort)
 
         hq = keep.tile([P, T + SLOTS], U32, name="hq", align_bytes=64)
         hs = keep.tile([P, T + SLOTS], U8, name="hs", align_bytes=64)
 
-        def first_layer(j, words, scales, e):
+        def operands(j):
+            if j < QUARTERS:
+                cols = slice(j * P, (j + 1) * P)
+                return [xw[:, o, cols] for o in range(PASSES)], [xs[:, o, cols] for o in range(PASSES)], SHARED
+            e = ORDER[j - QUARTERS]
+            cols = slice((e % 2) * C, (e % 2 + 1) * C)
+            return [gw[(e // 2, o)][:, cols] for o in range(PASSES)], [gs[(e // 2, o)][:, cols] for o in range(PASSES)], e
+
+        def product(acc, j, weights, planes):
+            words, scales, e = operands(j)
             g = [e in group for group in GROUPS].index(True)
-            planes = (s1[g], s3[g])
             first = (e - GROUPS[g].start) * PASSES
-            a = psum.tile([P, H], F32, name="a", tag=A_BANK[j])
+            for o in range(PASSES):
+                nc.tensor.matmul_mx(
+                    out=acc[:],
+                    lhsT=words[o].bitcast(FP8X4),
+                    lhsT_scale=scales[o],
+                    rhs=weights(e, o).bitcast(FP4X4),
+                    rhs_scale=planes[g][:, first + o, :],
+                    start=(o == 0),
+                    stop=(o == PASSES - 1),
+                )
+
+        def w1_of(e, o):
+            return w1_shared[:, o, :] if e == SHARED else w1[e // 2][:, (e % 2) * PASSES + o, :]
+
+        relu_a = {}
+        hidden = {}
+
+        def first_factor(j):
+            a = psum.tile([P, H], F32, name="a", tag="a%d" % (j % 3))
+            product(a, j, w1_of, s1)
+            relu_a[j] = reuse.tile([P, 2, P, 2], F32, name="relu_a%d" % j, align_bytes=64, offset=j * 4 * H)
+            nc.scalar.activation(relu_a[j][:], a[:].rearrange("p (m u d) -> p u m d", u=2, d=2), RELU)
+
+        def second_factor(j):
             b = psum.tile([P, H], F32, name="b", tag="b%d" % (j % 3))
-            for acc, w, plane in ((a, w1[e], planes[0]), (b, w3[e], planes[1])):
-                for o in range(PASSES):
-                    nc.tensor.matmul_mx(
-                        out=acc[:],
-                        lhsT=words[o].bitcast(FP8X4),
-                        lhsT_scale=scales[o],
-                        rhs=w[:, o, :].bitcast(FP4X4),
-                        rhs_scale=plane[:, first + o, :],
-                        start=(o == 0),
-                        stop=(o == PASSES - 1),
-                    )
-            relu_a = ring.tile([P, 2, P, 2], F32, name="relu_a", align_bytes=64)
-            nc.scalar.activation(relu_a[:], a[:].rearrange("p (m u d) -> p u m d", u=2, d=2), RELU)
-            h = ring.tile([P, 2, P, 2], BF16, name="h", bufs=4)
-            nc.vector.tensor_tensor(h[:], b[:].rearrange("p (m u d) -> p u m d", u=2, d=2), relu_a[:], MULT)
-            return h
+            product(b, j, lambda e, o: w3[e][:, o, :], s3)
+            hidden[j] = ring.tile([P, 2, P, 2], BF16, name="h", bufs=6)
+            nc.vector.tensor_tensor(hidden[j][:], b[:].rearrange("p (m u d) -> p u m d", u=2, d=2), relu_a[j][:], MULT)
+            for key, (job, offset) in LATE.items():
+                if job == j:
+                    gather(*key)
 
         def turn_and_quantize(tiles, codes, scales, bank):
             count = len(tiles)
@@ -146,32 +179,26 @@ def tile_moe_shr_glu_relu_kernel(
                 in_=grouped[:, 0:count, :, :].rearrange("p j c u -> p (j c u)").bitcast(BF16),
             )
 
-        per_chunk = GATHER // C
-
-        def operands(j):
-            kind, n = JOBS[j]
-            if kind == "s":
-                cols = slice(n * P, (n + 1) * P)
-                return [xw[:, o, cols] for o in range(PASSES)], [xs[:, o, cols] for o in range(PASSES)], SHARED
-            c = n // per_chunk
-            if n % per_chunk == 0:
-                gather(c)
-            cols = slice((n % per_chunk) * C, (n % per_chunk + 1) * C)
-            return [gw[c][o][:, cols] for o in range(PASSES)], [gs[c][o][:, cols] for o in range(PASSES)], n
-
         def quantize_group(first, count, bank):
             cols = slice(first * P, (first + count) * P)
-            turn_and_quantize(hidden[first : first + count], hq[:, cols], hs[:, cols], bank)
+            turn_and_quantize([hidden[j] for j in range(first, first + count)], hq[:, cols], hs[:, cols], bank)
 
-        hidden = []
-        last = len(JOBS) - 1
-        for j in range(len(JOBS)):
-            hidden.append(first_layer(j, *operands(j)))
-            if j == last:
-                quantize_group(j - 1, 1, A_BANK[j])
-            elif j % 2 == 0 and j > 0:
-                quantize_group(j - 2, 2, A_BANK[j])
-        quantize_group(last, 1, "b1")
+        for j in range(QUARTERS):
+            first_factor(j)
+        for j in range(QUARTERS):
+            second_factor(j)
+        quantize_group(0, 2, "t0")
+        for j in range(QUARTERS, QUARTERS + E, 2):
+            first_factor(j)
+            first_factor(j + 1)
+            if j == QUARTERS:
+                quantize_group(j - 2, 2, "t1")
+            second_factor(j)
+            second_factor(j + 1)
+            if j > QUARTERS:
+                quantize_group(j - 2, 2, "t%d" % ((j // 2 + 1) % 2))
+        quantize_group(QUARTERS + E - 2, 1, "t1")
+        quantize_group(QUARTERS + E - 1, 1, "a0")
 
         def second_layer(acc, e, codes, scales):
             nc.tensor.matmul_mx(
@@ -189,18 +216,16 @@ def tile_moe_shr_glu_relu_kernel(
         def routed_results(experts, tag, copy):
             acc = psum.tile([P, H], F32, name="y_acc", tag=tag)
             for i, e in enumerate(experts):
-                j = JOBS.index(("e", e))
+                j = QUARTERS + ORDER.index(e)
                 cols = slice(j * P, (j + 1) * P)
                 second_layer(acc[:, i * C : (i + 1) * C], e, hq[:, cols], hs[:, cols])
             copy(y[:, experts[0] * C : (experts[-1] + 1) * C], acc[:, 0 : len(experts) * C])
 
-        routed_results([7], "b0", nc.vector.tensor_copy)
-        routed_results([0, 1, 2, 3], "a2", nc.scalar.copy)
-        routed_results([4, 5, 6], "a3", nc.scalar.copy)
-        y_shared = psum.tile([P, T], F32, name="y_shared", tag="a0")
-        for first_token, first_col, width in ((0, 0, 2 * P), (2 * P, 2 * P, P), (3 * P, JOBS.index(("s", 3)) * P, P)):
-            cols = slice(first_col, first_col + width)
-            second_layer(y_shared[:, first_token : first_token + width], SHARED, hq[:, cols], hs[:, cols])
+        routed_results([4, 5, 6, 7], "b0", nc.scalar.copy)
+        routed_results([1, 2, 3], "a2", nc.scalar.copy)
+        routed_results([0], "b1", nc.vector.tensor_copy)
+        y_shared = psum.tile([P, T], F32, name="y_shared", tag="a1")
+        second_layer(y_shared[:], SHARED, hq[:, 0:T], hs[:, 0:T])
 
         first = keep.tile([P, T], F32, name="first")
         second = keep.tile([P, T], F32, name="second")

@@ -79,12 +79,13 @@ def tile_moe_shr_glu_relu_kernel(
         load_group_plane(nc.sync, s1, w1_scales, 0)
         load_words(w3[SHARED], w3_words[SHARED])
         load_group_plane(nc.sync, s3, w3_scales, 0)
-        load_group_plane(nc.gpsimd, s1, w1_scales, 1)
-        load_group_plane(nc.gpsimd, s3, w3_scales, 1)
         for i, e in enumerate(ORDER):
             if i % 2 == 0:
                 c = e // 2
                 load_words(w1[c], w1_words[2 * c : 2 * c + 2].rearrange("e s p c -> (e s) p c"))
+            if i == 0:
+                load_group_plane(nc.sync, s1, w1_scales, 1)
+                load_group_plane(nc.sync, s3, w3_scales, 1)
             load_words(w3[e], w3_words[e])
         load_words(w2, w2_words.rearrange("e s p c -> (e s) p c"))
         load_plane(nc.sync, s2, w2_scales.rearrange("e s f c -> (e s) f c"))
@@ -222,8 +223,8 @@ def tile_moe_shr_glu_relu_kernel(
             copy(y[:, experts[0] * C : (experts[-1] + 1) * C], acc[:, 0 : len(experts) * C])
 
         routed_results([4, 5, 6, 7], "b0", nc.scalar.copy)
-        routed_results([1, 2, 3], "a2", nc.scalar.copy)
-        routed_results([0], "b1", nc.vector.tensor_copy)
+        routed_results([2, 3], "a2", nc.scalar.copy)
+        routed_results([0, 1], "b1", nc.vector.tensor_copy)
         y_shared = psum.tile([P, T], F32, name="y_shared", tag="a1")
         second_layer(y_shared[:], SHARED, hq[:, 0:T], hs[:, 0:T])
 

@@ -25,6 +25,7 @@ SHARED = E
 GATHER = 256
 HALF = T // 2
 GROUPS = (range(6, E + 1), range(0, 6))
+W3_GROUPS = (range(6, E + 1), range(3, 6), range(0, 3))
 ORDER = (7, 6, 5, 4, 3, 2, 1, 0)
 QUARTERS = T // P
 LATE = {(1, 1, "s"): (2, 0), (1, 1, "w"): (3, 0), (0, 0, "w"): (3, 1024), (0, 0, "s"): (5, 0), (0, 1, "w"): (5, 1024), (0, 1, "s"): (7, 0)}
@@ -56,20 +57,20 @@ def tile_moe_shr_glu_relu_kernel(
         w3 = [keep.tile([P, PASSES, 2 * H], U8, name="w3_%d" % e, align_bytes=64) for e in range(E + 1)]
         w2 = keep.tile([P, E + 1, 2 * N], U8, name="w2", align_bytes=64)
         s1 = [keep.tile([P, len(group) * PASSES, H], U8, name="s1_%d" % g, align_bytes=64) for g, group in enumerate(GROUPS)]
-        s3 = [keep.tile([P, len(group) * PASSES, H], U8, name="s3_%d" % g, align_bytes=64) for g, group in enumerate(GROUPS)]
+        s3 = [keep.tile([P, len(group) * PASSES, H], U8, name="s3_%d" % g, align_bytes=64) for g, group in enumerate(W3_GROUPS)]
         s2 = keep.tile([P, E + 1, N], U8, name="s2", align_bytes=64)
         gate_t = keep.tile([P, 2, T], F32, name="gate_t")
         ident = keep.tile([P, P], F32, name="ident")
 
-        for plane in (xs, s1[0], s3[0], s1[1], s3[1], s2):
+        for plane in (xs, s1[0], s3[0], s1[1], s3[1], s3[2], s2):
             nc.vector.memset(plane[:].bitcast(I32), 0)
         make_identity(nc, ident[:])
 
         def load_words(tile, words):
             nc.sync.dma_start(out=tile[:].bitcast(I32), in_=words.rearrange("s p c -> p s c").bitcast(I32))
 
-        def load_group_plane(queue, plane, scales, g):
-            experts = slice(GROUPS[g].start, GROUPS[g].stop)
+        def load_group_plane(queue, plane, scales, g, groups=GROUPS):
+            experts = slice(groups[g].start, groups[g].stop)
             load_plane(queue, plane[g], scales[experts].rearrange("e s f c -> (e s) f c"))
 
         nc.sync.dma_start(offs_t[:], offs)
@@ -85,7 +86,8 @@ def tile_moe_shr_glu_relu_kernel(
                 load_words(w1[c], w1_words[2 * c : 2 * c + 2].rearrange("e s p c -> (e s) p c"))
             if i == 0:
                 load_group_plane(nc.sync, s1, w1_scales, 1)
-                load_group_plane(nc.sync, s3, w3_scales, 1)
+                load_group_plane(nc.sync, s3, w3_scales, 1, W3_GROUPS)
+                load_group_plane(nc.sync, s3, w3_scales, 2, W3_GROUPS)
             load_words(w3[e], w3_words[e])
         load_words(w2, w2_words.rearrange("e s p c -> (e s) p c"))
         load_plane(nc.sync, s2, w2_scales.rearrange("e s f c -> (e s) f c"))
@@ -129,10 +131,10 @@ def tile_moe_shr_glu_relu_kernel(
             cols = slice((e % 2) * C, (e % 2 + 1) * C)
             return [gw[(e // 2, o)][:, cols] for o in range(PASSES)], [gs[(e // 2, o)][:, cols] for o in range(PASSES)], e
 
-        def product(acc, j, weights, planes):
+        def product(acc, j, weights, planes, groups):
             words, scales, e = operands(j)
-            g = [e in group for group in GROUPS].index(True)
-            first = (e - GROUPS[g].start) * PASSES
+            g = [e in group for group in groups].index(True)
+            first = (e - groups[g].start) * PASSES
             for o in range(PASSES):
                 nc.tensor.matmul_mx(
                     out=acc[:],
@@ -152,13 +154,13 @@ def tile_moe_shr_glu_relu_kernel(
 
         def first_factor(j):
             a = psum.tile([P, H], F32, name="a", tag="a%d" % (j % 3))
-            product(a, j, w1_of, s1)
+            product(a, j, w1_of, s1, GROUPS)
             relu_a[j] = reuse.tile([P, 2, P, 2], F32, name="relu_a%d" % j, align_bytes=64, offset=j * 4 * H)
             nc.scalar.activation(relu_a[j][:], a[:].rearrange("p (m u d) -> p u m d", u=2, d=2), RELU)
 
         def second_factor(j):
             b = psum.tile([P, H], F32, name="b", tag="b%d" % (j % 3))
-            product(b, j, lambda e, o: w3[e][:, o, :], s3)
+            product(b, j, lambda e, o: w3[e][:, o, :], s3, W3_GROUPS)
             hidden[j] = ring.tile([P, 2, P, 2], BF16, name="h", bufs=6)
             nc.vector.tensor_tensor(hidden[j][:], b[:].rearrange("p (m u d) -> p u m d", u=2, d=2), relu_a[j][:], MULT)
             for key, (job, offset) in LATE.items():

@@ -24,16 +24,16 @@ SLOTS = E * C
 SHARED = E
 GATHER = 256
 HALF = T // 2
-GROUPS = (range(6, E + 1), range(0, 6))
-W3_GROUPS = (range(6, E + 1), range(3, 6), range(0, 3))
-ORDER = (7, 6, 5, 4, 3, 2, 1, 0)
 QUARTERS = T // P
-LATE = {(1, 1, "s"): (2, 0), (1, 1, "w"): (3, 0), (0, 0, "w"): (3, 1024), (0, 0, "s"): (5, 0), (0, 1, "w"): (5, 1024), (0, 1, "s"): (7, 0)}
+JOBS = QUARTERS + E
+W1_GROUPS = (range(6, E + 1), range(0, 6))
+W3_GROUPS = (range(6, E + 1), range(3, 6), range(0, 3))
+REGION = 4 * H
 
 
-def load_plane(queue, plane, rows):
+def load_rows(queue, plane, rows, which):
     by_row = rows.rearrange("m (q r) c -> r q m c", r=4)
-    for r in range(4):
+    for r in which:
         queue.dma_start(out=plane[r:P:32, :, :].bitcast(I32), in_=by_row[r].bitcast(I32))
 
 
@@ -47,193 +47,244 @@ def tile_moe_shr_glu_relu_kernel(
         reuse = ctx.enter_context(tc.tile_pool(name="reuse", bufs=1))
         psum = ctx.enter_context(tc.psum_pool(name="psum", bufs=1))
 
+        def shared_bytes(shape, dtype, name, region):
+            return reuse.tile(shape, dtype, name=name, align_bytes=64, offset=region * REGION)
+
+        def expert_of(job):
+            return SHARED if job < QUARTERS else JOBS - 1 - job
+
         offs_t = keep.tile([P, SLOTS // 16], U16, name="offs_t")
         pos1_t = keep.tile([P, T // 16], U16, name="pos1_t")
         pos2_t = keep.tile([P, T // 16], U16, name="pos2_t")
-        xw = keep.tile([P, PASSES, T], U32, name="xw", align_bytes=64)
+        xw = [keep.tile([P, T], U32, name="xw%d" % o, align_bytes=64) for o in range(PASSES)]
         xs = keep.tile([P, PASSES, T], U8, name="xs", align_bytes=64)
-        w1 = [keep.tile([P, 2 * PASSES, 2 * H], U8, name="w1_%d" % c, align_bytes=64) for c in range(E // 2)]
-        w1_shared = keep.tile([P, PASSES, 2 * H], U8, name="w1_shared", align_bytes=64)
-        w3 = [keep.tile([P, PASSES, 2 * H], U8, name="w3_%d" % e, align_bytes=64) for e in range(E + 1)]
+        w1 = [keep.tile([P, 2 * PASSES, 2 * H], U8, name="w1_%d" % c, align_bytes=64) for c in range(E // 2 - 1)]
+        w1.append(shared_bytes([P, 2 * PASSES, 2 * H], U8, "w1_first", JOBS + 2))
+        w1_shared = shared_bytes([P, PASSES, 2 * H], U8, "w1_shared", JOBS)
+        w3 = [keep.tile([P, PASSES, 2 * H], U8, name="w3_%d" % e, align_bytes=64) for e in range(E - 1)]
+        w3.append(shared_bytes([P, PASSES, 2 * H], U8, "w3_first", JOBS + 4))
+        w3.append(shared_bytes([P, PASSES, 2 * H], U8, "w3_shared", JOBS + 1))
         w2 = keep.tile([P, E + 1, 2 * N], U8, name="w2", align_bytes=64)
-        s1 = [keep.tile([P, len(group) * PASSES, H], U8, name="s1_%d" % g, align_bytes=64) for g, group in enumerate(GROUPS)]
-        s3 = [keep.tile([P, len(group) * PASSES, H], U8, name="s3_%d" % g, align_bytes=64) for g, group in enumerate(W3_GROUPS)]
-        s2 = keep.tile([P, E + 1, N], U8, name="s2", align_bytes=64)
-        gate_t = keep.tile([P, 2, T], F32, name="gate_t")
+        s1 = [keep.tile([P, len(group) * PASSES, H], U8, name="s1_%d" % g, align_bytes=64) for g, group in enumerate(W1_GROUPS)]
+        s3 = [keep.tile([P, len(group) * PASSES, H], U8, name="s3_%d" % g, align_bytes=64) for g, group in enumerate(W3_GROUPS[:1])]
+        gate1 = keep.tile([P, T], F32, name="gate1")
+        gate2 = keep.tile([P, T], F32, name="gate2")
         ident = keep.tile([P, P], F32, name="ident")
 
-        for plane in (xs, s1[0], s3[0], s1[1], s3[1], s3[2], s2):
+        for plane in (xs, s1[0], s3[0], s1[1]):
             nc.vector.memset(plane[:].bitcast(I32), 0)
         make_identity(nc, ident[:])
 
         def load_words(tile, words):
             nc.sync.dma_start(out=tile[:].bitcast(I32), in_=words.rearrange("s p c -> p s c").bitcast(I32))
 
-        def load_group_plane(queue, plane, scales, g, groups=GROUPS):
-            experts = slice(groups[g].start, groups[g].stop)
-            load_plane(queue, plane[g], scales[experts].rearrange("e s f c -> (e s) f c"))
+        def load_tokens(o):
+            nc.sync.dma_start(out=xw[o][:].bitcast(I32), in_=x_words[o].rearrange("p t r -> p (t r)").bitcast(I32))
+
+        def load_group(plane, scales, group):
+            load_rows(nc.sync, plane, scales[group.start : group.stop].rearrange("e s f c -> (e s) f c"), range(4))
+
+        def load_w1_pair(c):
+            load_words(w1[c], w1_words[2 * c : 2 * c + 2].rearrange("e s p c -> (e s) p c"))
+
+        def load_w1_single(e):
+            nc.sync.dma_start(
+                out=w1[e // 2][:, (e % 2) * PASSES : (e % 2 + 1) * PASSES, :].bitcast(I32),
+                in_=w1_words[e].rearrange("s p c -> p s c").bitcast(I32),
+            )
 
         nc.sync.dma_start(offs_t[:], offs)
-        nc.sync.dma_start(out=xw[:].bitcast(I32), in_=x_words.rearrange("o p t r -> p o (t r)").bitcast(I32))
-        load_plane(nc.sync, xs, x_scales)
+        load_tokens(0)
+        load_rows(nc.sync, xs, x_scales, range(4))
         load_words(w1_shared, w1_words[SHARED])
-        load_group_plane(nc.sync, s1, w1_scales, 0)
+        load_group(s1[0], w1_scales, W1_GROUPS[0])
+        load_group(s3[0], w3_scales, W3_GROUPS[0])
+        load_tokens(1)
         load_words(w3[SHARED], w3_words[SHARED])
-        load_group_plane(nc.sync, s3, w3_scales, 0)
-        for i, e in enumerate(ORDER):
-            if i % 2 == 0:
-                c = e // 2
-                load_words(w1[c], w1_words[2 * c : 2 * c + 2].rearrange("e s p c -> (e s) p c"))
-            if i == 0:
-                load_group_plane(nc.sync, s1, w1_scales, 1)
-                load_group_plane(nc.sync, s3, w3_scales, 1, W3_GROUPS)
-                load_group_plane(nc.sync, s3, w3_scales, 2, W3_GROUPS)
-            load_words(w3[e], w3_words[e])
-        load_words(w2, w2_words.rearrange("e s p c -> (e s) p c"))
-        load_plane(nc.sync, s2, w2_scales.rearrange("e s f c -> (e s) f c"))
-        nc.sync.dma_start(pos1_t[:], pos1)
-        nc.sync.dma_start(pos2_t[:], pos2)
-        nc.sync.dma_start(out=gate_t[:], in_=gate.rearrange("r p t -> p r t"))
+        load_w1_pair(3)
+        load_words(w3[7], w3_words[7])
+        load_words(w3[6], w3_words[6])
+        load_w1_pair(2)
+        load_group(s1[1], w1_scales, W1_GROUPS[1])
 
-        gw = {}
-        gs = {}
+        gathered = {}
 
-        def gathered_tile(c, o, sort, dtype):
-            name = "g%s%d_%d" % (sort, c, o)
-            if (c, o, sort) in LATE:
-                j, offset = LATE[(c, o, sort)]
-                return reuse.tile([P, GATHER], dtype, name=name, align_bytes=64, offset=j * 4 * H + offset)
-            return keep.tile([P, GATHER], dtype, name=name, align_bytes=64)
-
-        def gather(c, o, sort):
+        def gather(c, o, sort, behind=None, offset=0):
             entries = offs_t[:, c * GATHER // 16 : (c + 1) * GATHER // 16]
-            if sort == "w":
-                gw[(c, o)] = gathered_tile(c, o, sort, U32)
-                nc.vector.tensor_copy(gw[(c, o)][:], xw[:, o, :].indirect(entries))
+            name = "g%s%d_%d" % (sort, c, o)
+            dtype = U32 if sort == "w" else U8
+            if behind is None:
+                tile = keep.tile([P, GATHER], dtype, name=name, align_bytes=64)
             else:
-                gs[(c, o)] = gathered_tile(c, o, sort, U8)
-                nc.vector.tensor_copy(gs[(c, o)][:], xs[:, o, :].indirect(entries))
+                tile = reuse.tile([P, GATHER], dtype, name=name, align_bytes=64, offset=behind * REGION + offset)
+            window = xw[o][:] if sort == "w" else xs[:, o, :]
+            nc.vector.tensor_copy(tile[:], window.indirect(entries))
+            gathered[(c, o, sort)] = tile
 
         for c in (3, 2, 1, 0):
+            gather(c, 0, "w")
+        for c in (3, 2):
             for o in range(PASSES):
-                for sort in ("w", "s"):
-                    if (c, o, sort) not in LATE:
-                        gather(c, o, sort)
+                gather(c, o, "s")
+        for c in (3, 2, 1):
+            gather(c, 1, "w")
+        held = {3: [(1, 0, "s"), (1, 1, "s")], 5: [(0, 1, "w"), (0, 0, "s")], 7: [(0, 1, "s")]}
 
-        hq = keep.tile([P, T + SLOTS], U32, name="hq", align_bytes=64)
-        hs = keep.tile([P, T + SLOTS], U8, name="hs", align_bytes=64)
-
-        def operands(j):
-            if j < QUARTERS:
-                cols = slice(j * P, (j + 1) * P)
-                return [xw[:, o, cols] for o in range(PASSES)], [xs[:, o, cols] for o in range(PASSES)], SHARED
-            e = ORDER[j - QUARTERS]
-            cols = slice((e % 2) * C, (e % 2 + 1) * C)
-            return [gw[(e // 2, o)][:, cols] for o in range(PASSES)], [gs[(e // 2, o)][:, cols] for o in range(PASSES)], e
-
-        def product(acc, j, weights, planes, groups):
-            words, scales, e = operands(j)
+        def one_pass(acc, job, o, weights, planes, groups):
+            e = expert_of(job)
+            if e == SHARED:
+                cols = slice(job * P, (job + 1) * P)
+                words, scales = xw[o][:, cols], xs[:, o, cols]
+            else:
+                cols = slice((e % 2) * C, (e % 2 + 1) * C)
+                words, scales = gathered[(e // 2, o, "w")][:, cols], gathered[(e // 2, o, "s")][:, cols]
             g = [e in group for group in groups].index(True)
-            first = (e - groups[g].start) * PASSES
-            for o in range(PASSES):
-                nc.tensor.matmul_mx(
-                    out=acc[:],
-                    lhsT=words[o].bitcast(FP8X4),
-                    lhsT_scale=scales[o],
-                    rhs=weights(e, o).bitcast(FP4X4),
-                    rhs_scale=planes[g][:, first + o, :],
-                    start=(o == 0),
-                    stop=(o == PASSES - 1),
-                )
+            nc.tensor.matmul_mx(
+                out=acc[:],
+                lhsT=words.bitcast(FP8X4),
+                lhsT_scale=scales,
+                rhs=weights.bitcast(FP4X4),
+                rhs_scale=planes[g][:, (e - groups[g].start) * PASSES + o, :],
+                start=(o == 0),
+                stop=(o == PASSES - 1),
+            )
 
-        def w1_of(e, o):
+        def w1_of(job, o):
+            e = expert_of(job)
             return w1_shared[:, o, :] if e == SHARED else w1[e // 2][:, (e % 2) * PASSES + o, :]
 
         relu_a = {}
         hidden = {}
+        codes = {}
 
-        def first_factor(j):
-            a = psum.tile([P, H], F32, name="a", tag="a%d" % (j % 3))
-            product(a, j, w1_of, s1, GROUPS)
-            relu_a[j] = reuse.tile([P, 2, P, 2], F32, name="relu_a%d" % j, align_bytes=64, offset=j * 4 * H)
-            nc.scalar.activation(relu_a[j][:], a[:].rearrange("p (m u d) -> p u m d", u=2, d=2), RELU)
+        def take_relu(job, a):
+            relu_a[job] = shared_bytes([P, 2, P, 2], F32, "relu_a%d" % job, job)
+            nc.scalar.activation(relu_a[job][:], a[:].rearrange("p (m u d) -> p u m d", u=2, d=2), RELU)
 
-        def second_factor(j):
-            b = psum.tile([P, H], F32, name="b", tag="b%d" % (j % 3))
-            product(b, j, lambda e, o: w3[e][:, o, :], s3, W3_GROUPS)
-            hidden[j] = ring.tile([P, 2, P, 2], BF16, name="h", bufs=6)
-            nc.vector.tensor_tensor(hidden[j][:], b[:].rearrange("p (m u d) -> p u m d", u=2, d=2), relu_a[j][:], MULT)
-            for key, (job, offset) in LATE.items():
-                if job == j:
-                    gather(*key)
+        def first_factor(job, bank):
+            a = psum.tile([P, H], F32, name="a", tag=bank)
+            for o in range(PASSES):
+                one_pass(a, job, o, w1_of(job, o), s1, W1_GROUPS)
+            take_relu(job, a)
 
-        def turn_and_quantize(tiles, codes, scales, bank):
-            count = len(tiles)
+        def second_factor(job, bank, behind=None):
+            b = psum.tile([P, H], F32, name="b", tag=bank)
+            for o in range(PASSES):
+                one_pass(b, job, o, w3[expert_of(job)][:, o, :], s3, W3_GROUPS)
+            if behind is None:
+                hidden[job] = ring.tile([P, 2, P, 2], BF16, name="h", bufs=6)
+            else:
+                hidden[job] = shared_bytes([P, 2, P, 2], BF16, "h%d" % job, behind)
+            nc.vector.tensor_tensor(hidden[job][:], b[:].rearrange("p (m u d) -> p u m d", u=2, d=2), relu_a[job][:], MULT)
+            for i, key in enumerate(held.get(job, [])):
+                gather(*key, behind=job, offset=i * REGION // 2)
+
+        def quantize(jobs, bank, grouped_in=None, codes_in=None, copy=nc.scalar.copy):
+            count = len(jobs)
             turned = psum.tile([P, 2, 2, P], F32, name="turned", tag=bank)
-            for j, h in enumerate(tiles):
-                pairs = h[:].rearrange("p u m d -> p u (m d)").bitcast(F32)
+            for i, job in enumerate(jobs):
+                pairs = hidden[job][:].rearrange("p u m d -> p u (m d)").bitcast(F32)
                 for u in range(2):
-                    nc.tensor.transpose(turned[:, j, u, :], pairs[:, u, :], ident[:])
-            grouped = ring.tile([P, 2, P, 2], F32, name="grouped", align_bytes=64)
-            nc.scalar.copy(grouped[:, 0:count, :, :], turned[:, 0:count, :, :].rearrange("p j u c -> p j c u"))
+                    nc.tensor.transpose(turned[:, i, u, :], pairs[:, u, :], ident[:])
+            if grouped_in is None:
+                grouped = ring.tile([P, 2, P, 2], F32, name="grouped", align_bytes=64)
+            else:
+                grouped = shared_bytes([P, 1, P, 2], F32, "grouped%d" % jobs[0], grouped_in)
+            copy(grouped[:, 0:count, :, :], turned[:, 0:count, :, :].rearrange("p j u c -> p j c u"))
+            if codes_in is None:
+                words = keep.tile([P, count * P], U32, name="hq%d" % jobs[0], align_bytes=64)
+            else:
+                words = shared_bytes([P, count * P], U32, "hq%d" % jobs[0], codes_in)
+            scales = keep.tile([P, count * P], U8, name="hs%d" % jobs[0], align_bytes=64)
             nc.vector.quantize_mx(
-                out=codes.bitcast(FP8X4),
-                scales=scales,
+                out=words[:].bitcast(FP8X4),
+                scales=scales[:],
                 in_=grouped[:, 0:count, :, :].rearrange("p j c u -> p (j c u)").bitcast(BF16),
             )
+            for i, job in enumerate(jobs):
+                codes[job] = (words[:, i * P : (i + 1) * P], scales[:, i * P : (i + 1) * P])
 
-        def quantize_group(first, count, bank):
-            cols = slice(first * P, (first + count) * P)
-            turn_and_quantize([hidden[j] for j in range(first, first + count)], hq[:, cols], hs[:, cols], bank)
-
-        for j in range(QUARTERS):
-            first_factor(j)
-        for j in range(QUARTERS):
-            second_factor(j)
-        quantize_group(0, 2, "t0")
-        for j in range(QUARTERS, QUARTERS + E, 2):
-            first_factor(j)
-            first_factor(j + 1)
-            if j == QUARTERS:
-                quantize_group(j - 2, 2, "t1")
-            second_factor(j)
-            second_factor(j + 1)
-            if j > QUARTERS:
-                quantize_group(j - 2, 2, "t%d" % ((j // 2 + 1) % 2))
-        quantize_group(QUARTERS + E - 2, 1, "t1")
-        quantize_group(QUARTERS + E - 1, 1, "a0")
-
-        def second_layer(acc, e, codes, scales):
+        def second_layer(acc, job):
+            e = expert_of(job)
             nc.tensor.matmul_mx(
                 out=acc,
                 lhsT=w2[:, e, :].bitcast(FP4X4),
                 lhsT_scale=s2[:, e, :],
-                rhs=codes.bitcast(FP8X4),
-                rhs_scale=scales,
+                rhs=codes[job][0].bitcast(FP8X4),
+                rhs_scale=codes[job][1],
                 start=True,
                 stop=True,
             )
 
         y = keep.tile([P, SLOTS], F32, name="y")
 
-        def routed_results(experts, tag, copy):
-            acc = psum.tile([P, H], F32, name="y_acc", tag=tag)
+        def routed_results(experts, bank, copy):
+            acc = psum.tile([P, H], F32, name="y_acc", tag=bank)
             for i, e in enumerate(experts):
-                j = QUARTERS + ORDER.index(e)
-                cols = slice(j * P, (j + 1) * P)
-                second_layer(acc[:, i * C : (i + 1) * C], e, hq[:, cols], hs[:, cols])
+                second_layer(acc[:, i * C : (i + 1) * C], JOBS - 1 - e)
             copy(y[:, experts[0] * C : (experts[-1] + 1) * C], acc[:, 0 : len(experts) * C])
 
+        shared_a = [psum.tile([P, H], F32, name="a", tag="a%d" % job) for job in range(QUARTERS)]
+        for o in range(PASSES):
+            for job in range(QUARTERS):
+                one_pass(shared_a[job], job, o, w1_of(job, o), s1, W1_GROUPS)
+        for job in range(QUARTERS):
+            take_relu(job, shared_a[job])
+        for job in range(QUARTERS):
+            second_factor(job, "b%d" % job)
+        first_factor(4, "a0")
+        first_factor(5, "a1")
+        second_factor(4, "b0")
+        second_factor(5, "b1")
+        for g, region in ((1, JOBS), (2, JOBS + 2)):
+            s3.append(shared_bytes([P, len(W3_GROUPS[g]) * PASSES, H], U8, "s3_%d" % g, region))
+        s2 = shared_bytes([P, E + 1, N], U8, "s2", JOBS + 4)
+        load_group(s3[1], w3_scales, W3_GROUPS[1])
+        load_group(s3[2], w3_scales, W3_GROUPS[2])
+        load_words(w3[5], w3_words[5])
+        load_words(w3[4], w3_words[4])
+        for pair in ((3, 2), (1, 0)):
+            for e in pair:
+                load_w1_single(e)
+            for e in pair:
+                load_words(w3[e], w3_words[e])
+        load_words(w2, w2_words.rearrange("e s p c -> (e s) p c"))
+        load_rows(nc.sync, s2, w2_scales.rearrange("e s f c -> (e s) f c"), range(4))
+        nc.sync.dma_start(pos1_t[:], pos1)
+        nc.sync.dma_start(pos2_t[:], pos2)
+        nc.sync.dma_start(out=gate1[:], in_=gate[0])
+        nc.sync.dma_start(out=gate2[:], in_=gate[1])
+        quantize([0, 1], "a2")
+        quantize([2, 3], "a3")
+        first_factor(6, "a0")
+        first_factor(7, "a1")
+        quantize([4, 5], "a0")
+        second_factor(6, "b2")
+        second_factor(7, "b3")
+        first_factor(8, "a2")
+        first_factor(9, "a3")
+        second_factor(8, "b0")
+        second_factor(9, "b1")
+        quantize([6, 7], "a3")
+        first_factor(10, "a1")
+        first_factor(11, "a0")
+        second_factor(10, "b2")
+        second_factor(11, "b3")
+        quantize([8, 9], "a0")
+        quantize([10], "a2", copy=nc.vector.tensor_copy)
+        quantize([11], "a1")
         routed_results([4, 5, 6, 7], "b0", nc.scalar.copy)
-        routed_results([2, 3], "a2", nc.scalar.copy)
-        routed_results([0, 1], "b1", nc.vector.tensor_copy)
-        y_shared = psum.tile([P, T], F32, name="y_shared", tag="a1")
-        second_layer(y_shared[:], SHARED, hq[:, 0:T], hs[:, 0:T])
+        routed_results([2, 3], "a3", nc.vector.tensor_copy)
+        routed_results([1], "b1", nc.scalar.copy)
+        routed_results([0], "a2", nc.vector.tensor_copy)
+        y_shared = psum.tile([P, T], F32, name="y_shared", tag="b2")
+        for job in range(QUARTERS):
+            second_layer(y_shared[:, job * P : (job + 1) * P], job)
 
         first = keep.tile([P, T], F32, name="first")
         second = keep.tile([P, T], F32, name="second")
-        nc.vector.tensor_tensor(first[:], y[:].indirect(pos1_t[:]), gate_t[:, 0, :], MULT)
-        nc.vector.tensor_tensor(second[:], y[:].indirect(pos2_t[:]), gate_t[:, 1, :], MULT)
+        nc.vector.tensor_tensor(first[:], y[:].indirect(pos1_t[:]), gate1[:], MULT)
+        nc.vector.tensor_tensor(second[:], y[:].indirect(pos2_t[:]), gate2[:], MULT)
         halves = [slice(half * HALF, (half + 1) * HALF) for half in range(2)]
         partial = keep.tile([P, T], F32, name="partial")
         total = keep.tile([P, T], F32, name="total")

@@ -26,7 +26,7 @@ GATHER = 256
 HALF = T // 2
 QUARTERS = T // P
 JOBS = QUARTERS + E
-W1_GROUPS = (range(6, E + 1), range(0, 6))
+W1_GROUPS = (range(6, E + 1), range(4, 6), range(0, 4))
 W3_GROUPS = (range(6, E + 1), range(3, 6), range(0, 3))
 REGION = 4 * H
 
@@ -65,13 +65,13 @@ def tile_moe_shr_glu_relu_kernel(
         w3.append(shared_bytes([P, PASSES, 2 * H], U8, "w3_first", JOBS + 4))
         w3.append(shared_bytes([P, PASSES, 2 * H], U8, "w3_shared", JOBS + 1))
         w2 = keep.tile([P, E + 1, 2 * N], U8, name="w2", align_bytes=64)
-        s1 = [keep.tile([P, len(group) * PASSES, H], U8, name="s1_%d" % g, align_bytes=64) for g, group in enumerate(W1_GROUPS)]
-        s3 = [keep.tile([P, len(group) * PASSES, H], U8, name="s3_%d" % g, align_bytes=64) for g, group in enumerate(W3_GROUPS[:1])]
+        s1 = [keep.tile([P, len(group) * PASSES, H], U8, name="s1_%d" % g, align_bytes=64) for g, group in enumerate(W1_GROUPS[:2])]
+        s3 = [keep.tile([P, len(group) * PASSES, H], U8, name="s3_%d" % g, align_bytes=64) for g, group in enumerate(W3_GROUPS[:2])]
         gate1 = keep.tile([P, T], F32, name="gate1")
         gate2 = keep.tile([P, T], F32, name="gate2")
         ident = keep.tile([P, P], F32, name="ident")
 
-        for plane in (xs, s1[0], s3[0], s1[1]):
+        for plane in (xs, s1[0], s3[0], s3[1], s1[1]):
             nc.vector.memset(plane[:].bitcast(I32), 0)
         make_identity(nc, ident[:])
 
@@ -105,7 +105,8 @@ def tile_moe_shr_glu_relu_kernel(
         load_words(w3[7], w3_words[7])
         load_words(w3[6], w3_words[6])
         load_w1_pair(2)
-        load_group(s1[1], w1_scales, W1_GROUPS[1])
+        load_words(w3[5], w3_words[5])
+        load_words(w3[4], w3_words[4])
 
         gathered = {}
 
@@ -236,13 +237,13 @@ def tile_moe_shr_glu_relu_kernel(
         first_factor(5, "a1")
         second_factor(4, "b0")
         second_factor(5, "b1")
-        for g, region in ((1, JOBS), (2, JOBS + 2)):
-            s3.append(shared_bytes([P, len(W3_GROUPS[g]) * PASSES, H], U8, "s3_%d" % g, region))
+        s1.append(shared_bytes([P, len(W1_GROUPS[2]) * PASSES, H], U8, "s1_2", JOBS))
+        s3.append(shared_bytes([P, len(W3_GROUPS[2]) * PASSES, H], U8, "s3_2", JOBS + 2))
         s2 = shared_bytes([P, E + 1, N], U8, "s2", JOBS + 4)
         load_group(s3[1], w3_scales, W3_GROUPS[1])
+        load_group(s1[1], w1_scales, W1_GROUPS[1])
+        load_group(s1[2], w1_scales, W1_GROUPS[2])
         load_group(s3[2], w3_scales, W3_GROUPS[2])
-        load_words(w3[5], w3_words[5])
-        load_words(w3[4], w3_words[4])
         for pair in ((3, 2), (1, 0)):
             for e in pair:
                 load_w1_single(e)
@@ -258,9 +259,9 @@ def tile_moe_shr_glu_relu_kernel(
         quantize([2, 3], "a3")
         first_factor(6, "a0")
         first_factor(7, "a1")
-        quantize([4, 5], "a0")
         second_factor(6, "b2")
         second_factor(7, "b3")
+        quantize([4, 5], "a0")
         first_factor(8, "a2")
         first_factor(9, "a3")
         second_factor(8, "b0")

@@ -67,8 +67,8 @@ def tile_moe_shr_glu_relu_kernel(
         w2 = keep.tile([P, E + 1, 2 * N], U8, name="w2", align_bytes=64)
         s1 = [keep.tile([P, len(group) * PASSES, H], U8, name="s1_%d" % g, align_bytes=64) for g, group in enumerate(W1_GROUPS[:2])]
         s3 = [keep.tile([P, len(group) * PASSES, H], U8, name="s3_%d" % g, align_bytes=64) for g, group in enumerate(W3_GROUPS[:2])]
-        gate1 = keep.tile([P, T], F32, name="gate1")
-        gate2 = keep.tile([P, T], F32, name="gate2")
+        gates = keep.tile([P, 2, T], F32, name="gates")
+        gate1, gate2 = gates[:, 0, :], gates[:, 1, :]
         ident = keep.tile([P, P], F32, name="ident")
 
         for plane in (xs, s1[0], s3[0], s3[1], s1[1]):
@@ -253,8 +253,7 @@ def tile_moe_shr_glu_relu_kernel(
         load_rows(nc.sync, s2, w2_scales.rearrange("e s f c -> (e s) f c"), range(4))
         nc.sync.dma_start(pos1_t[:], pos1)
         nc.sync.dma_start(pos2_t[:], pos2)
-        nc.sync.dma_start(out=gate1[:], in_=gate[0])
-        nc.sync.dma_start(out=gate2[:], in_=gate[1])
+        nc.sync.dma_start(out=gates[:], in_=gate.rearrange("g p t -> p g t"))
         quantize([0, 1], "a2")
         quantize([2, 3], "a3")
         first_factor(6, "a0")
@@ -282,15 +281,26 @@ def tile_moe_shr_glu_relu_kernel(
         for job in range(QUARTERS):
             second_layer(y_shared[:, job * P : (job + 1) * P], job)
 
+        copy_f = mybir.ActivationFunctionType.Copy
+        low, high = slice(0, HALF), slice(HALF, T)
+        low_entries, high_entries = slice(0, HALF // 16), slice(HALF // 16, T // 16)
+        second_low = keep.tile([P, HALF], F32, name="second_low")
+        first_high = keep.tile([P, HALF], F32, name="first_high")
+        second_high = keep.tile([P, HALF], F32, name="second_high")
+        nc.scalar.activation(second_low[:], y[:].indirect(pos2_t[:, low_entries]), copy_f)
+        nc.scalar.activation(first_high[:], y[:].indirect(pos1_t[:, high_entries]), copy_f)
+        nc.scalar.activation(second_high[:], y[:].indirect(pos2_t[:, high_entries]), copy_f)
         first = keep.tile([P, T], F32, name="first")
         second = keep.tile([P, T], F32, name="second")
-        nc.vector.tensor_tensor(first[:], y[:].indirect(pos1_t[:]), gate1[:], MULT)
-        nc.vector.tensor_tensor(second[:], y[:].indirect(pos2_t[:]), gate2[:], MULT)
-        halves = [slice(half * HALF, (half + 1) * HALF) for half in range(2)]
         partial = keep.tile([P, T], F32, name="partial")
         total = keep.tile([P, T], F32, name="total")
-        for cols in halves:
-            nc.vector.tensor_tensor(partial[:, cols], y_shared[:, cols], first[:, cols], ADD)
-        for cols in halves:
-            nc.vector.tensor_tensor(total[:, cols], partial[:, cols], second[:, cols], ADD)
-            nc.sync.dma_start(out=out[:, cols], in_=total[:, cols])
+        nc.vector.tensor_tensor(first[:, low], y[:].indirect(pos1_t[:, low_entries]), gate1[:, low], MULT)
+        nc.vector.tensor_tensor(second[:, low], second_low[:], gate2[:, low], MULT)
+        nc.vector.tensor_tensor(partial[:, low], y_shared[:, low], first[:, low], ADD)
+        nc.vector.tensor_tensor(first[:, high], first_high[:], gate1[:, high], MULT)
+        nc.vector.tensor_tensor(total[:, low], partial[:, low], second[:, low], ADD)
+        nc.sync.dma_start(out=out[:, low], in_=total[:, low])
+        nc.vector.tensor_tensor(partial[:, high], y_shared[:, high], first[:, high], ADD)
+        nc.vector.tensor_tensor(second[:, high], second_high[:], gate2[:, high], MULT)
+        nc.vector.tensor_tensor(total[:, high], partial[:, high], second[:, high], ADD)
+        nc.sync.dma_start(out=out[:, high], in_=total[:, high])

@@ -93,8 +93,8 @@ def tile_moe_shr_glu_relu_kernel(
                 in_=w1_words[e].rearrange("s p c -> p s c").bitcast(I32),
             )
 
-        nc.sync.dma_start(offs_t[:], offs)
         load_tokens(0)
+        nc.sync.dma_start(offs_t[:], offs)
         load_rows(nc.sync, xs, x_scales, range(4))
         load_words(w1_shared, w1_words[SHARED])
         load_group(s1[0], w1_scales, W1_GROUPS[0])
@@ -289,7 +289,9 @@ def tile_moe_shr_glu_relu_kernel(
         second_high = keep.tile([P, HALF], F32, name="second_high")
         nc.scalar.activation(second_low[:], y[:].indirect(pos2_t[:, low_entries]), copy_f)
         nc.scalar.activation(first_high[:], y[:].indirect(pos1_t[:, high_entries]), copy_f)
-        nc.scalar.activation(second_high[:], y[:].indirect(pos2_t[:, high_entries]), copy_f)
+        for q in range(2):
+            entries = pos2_t[:, (HALF + q * P) // 16 : (HALF + (q + 1) * P) // 16]
+            nc.scalar.activation(second_high[:, q * P : (q + 1) * P], y[:].indirect(entries), copy_f)
         first = keep.tile([P, T], F32, name="first")
         second = keep.tile([P, T], F32, name="second")
         partial = keep.tile([P, T], F32, name="partial")
@@ -301,6 +303,9 @@ def tile_moe_shr_glu_relu_kernel(
         nc.vector.tensor_tensor(total[:, low], partial[:, low], second[:, low], ADD)
         nc.sync.dma_start(out=out[:, low], in_=total[:, low])
         nc.vector.tensor_tensor(partial[:, high], y_shared[:, high], first[:, high], ADD)
-        nc.vector.tensor_tensor(second[:, high], second_high[:], gate2[:, high], MULT)
-        nc.vector.tensor_tensor(total[:, high], partial[:, high], second[:, high], ADD)
-        nc.sync.dma_start(out=out[:, high], in_=total[:, high])
+        quarters = [slice(HALF + q * P, HALF + (q + 1) * P) for q in range(2)]
+        for q, cols in enumerate(quarters):
+            nc.vector.tensor_tensor(second[:, cols], second_high[:, q * P : (q + 1) * P], gate2[:, cols], MULT)
+        for cols in quarters:
+            nc.vector.tensor_tensor(total[:, cols], partial[:, cols], second[:, cols], ADD)
+            nc.sync.dma_start(out=out[:, cols], in_=total[:, cols])

@@ -69,11 +69,9 @@ def tile_moe_shr_glu_relu_kernel(
         s3 = [keep.tile([P, len(group) * PASSES, H], U8, name="s3_%d" % g, align_bytes=64) for g, group in enumerate(W3_GROUPS[:2])]
         gates = keep.tile([P, 2, T], F32, name="gates")
         gate1, gate2 = gates[:, 0, :], gates[:, 1, :]
-        ident = keep.tile([P, P], F32, name="ident")
 
         for plane in (xs, s1[0], s3[0], s3[1], s1[1]):
             nc.vector.memset(plane[:].bitcast(I32), 0)
-        make_identity(nc, ident[:])
 
         def load_words(tile, words):
             nc.sync.dma_start(out=tile[:].bitcast(I32), in_=words.rearrange("s p c -> p s c").bitcast(I32))
@@ -131,7 +129,7 @@ def tile_moe_shr_glu_relu_kernel(
             gather(c, 1, "w")
         held = {3: [(1, 0, "s"), (1, 1, "s")], 5: [(0, 1, "w"), (0, 0, "s")], 7: [(0, 1, "s")]}
 
-        def one_pass(acc, job, o, weights, planes, groups):
+        def one_pass(acc, job, o, weights, planes, groups, part=slice(0, H)):
             e = expert_of(job)
             if e == SHARED:
                 cols = slice(job * P, (job + 1) * P)
@@ -144,8 +142,8 @@ def tile_moe_shr_glu_relu_kernel(
                 out=acc[:],
                 lhsT=words.bitcast(FP8X4),
                 lhsT_scale=scales,
-                rhs=weights.bitcast(FP4X4),
-                rhs_scale=planes[g][:, (e - groups[g].start) * PASSES + o, :],
+                rhs=weights[:, 2 * part.start : 2 * part.stop].bitcast(FP4X4),
+                rhs_scale=planes[g][:, (e - groups[g].start) * PASSES + o, part],
                 start=(o == 0),
                 stop=(o == PASSES - 1),
             )
@@ -180,22 +178,30 @@ def tile_moe_shr_glu_relu_kernel(
             for i, key in enumerate(held.get(job, [])):
                 gather(*key, behind=job, offset=i * REGION // 2)
 
-        def quantize(jobs, bank, grouped_in=None, codes_in=None, copy=nc.scalar.copy):
+        def second_factor_in_halves(job, banks):
+            hidden[job] = ring.tile([P, 2, P, 2], BF16, name="h", bufs=6)
+            for half, bank in enumerate(banks):
+                b = psum.tile([P, H // 2], F32, name="b_half", tag=bank)
+                for o in range(PASSES):
+                    one_pass(b, job, o, w3[expert_of(job)][:, o, :], s3, W3_GROUPS, slice(half * H // 2, (half + 1) * H // 2))
+                words = slice(half * P // 2, (half + 1) * P // 2)
+                nc.vector.tensor_tensor(
+                    hidden[job][:, :, words, :], b[:].rearrange("p (m u d) -> p u m d", u=2, d=2), relu_a[job][:, :, words, :], MULT
+                )
+
+        def quantize(jobs, turns):
             count = len(jobs)
-            turned = psum.tile([P, 2, 2, P], F32, name="turned", tag=bank)
-            for i, job in enumerate(jobs):
-                pairs = hidden[job][:].rearrange("p u m d -> p u (m d)").bitcast(F32)
-                for u in range(2):
-                    nc.tensor.transpose(turned[:, i, u, :], pairs[:, u, :], ident[:])
-            if grouped_in is None:
-                grouped = ring.tile([P, 2, P, 2], F32, name="grouped", align_bytes=64)
-            else:
-                grouped = shared_bytes([P, 1, P, 2], F32, "grouped%d" % jobs[0], grouped_in)
-            copy(grouped[:, 0:count, :, :], turned[:, 0:count, :, :].rearrange("p j u c -> p j c u"))
-            if codes_in is None:
-                words = keep.tile([P, count * P], U32, name="hq%d" % jobs[0], align_bytes=64)
-            else:
-                words = shared_bytes([P, count * P], U32, "hq%d" % jobs[0], codes_in)
+            grouped = ring.tile([P, 2, P, 2], F32, name="grouped", align_bytes=64)
+            done = 0
+            for width, bank, copy in turns:
+                turned = psum.tile([P, 2, 2, P], F32, name="turned", tag=bank)
+                for i, job in enumerate(jobs[done : done + width]):
+                    pairs = hidden[job][:].rearrange("p u m d -> p u (m d)").bitcast(F32)
+                    for u in range(2):
+                        nc.tensor.transpose(turned[:, i, u, :], pairs[:, u, :], ident[:])
+                copy(grouped[:, done : done + width, :, :], turned[:, 0:width, :, :].rearrange("p j u c -> p j c u"))
+                done = done + width
+            words = keep.tile([P, count * P], U32, name="hq%d" % jobs[0], align_bytes=64)
             scales = keep.tile([P, count * P], U8, name="hs%d" % jobs[0], align_bytes=64)
             nc.vector.quantize_mx(
                 out=words[:].bitcast(FP8X4),
@@ -233,6 +239,8 @@ def tile_moe_shr_glu_relu_kernel(
             take_relu(job, shared_a[job])
         for job in range(QUARTERS):
             second_factor(job, "b%d" % job)
+        ident = shared_bytes([P, P], F32, "ident", 0)
+        make_identity(nc, ident[:])
         first_factor(4, "a0")
         first_factor(5, "a1")
         second_factor(4, "b0")
@@ -254,25 +262,25 @@ def tile_moe_shr_glu_relu_kernel(
         nc.sync.dma_start(pos1_t[:], pos1)
         nc.sync.dma_start(pos2_t[:], pos2)
         nc.sync.dma_start(out=gates[:], in_=gate.rearrange("g p t -> p g t"))
-        quantize([0, 1], "a2")
-        quantize([2, 3], "a3")
+        quantize([0, 1], [(2, "a2", nc.scalar.copy)])
+        quantize([2, 3], [(2, "a3", nc.scalar.copy)])
         first_factor(6, "a0")
         first_factor(7, "a1")
         second_factor(6, "b2")
         second_factor(7, "b3")
-        quantize([4, 5], "a0")
+        quantize([4, 5], [(2, "a0", nc.scalar.copy)])
         first_factor(8, "a2")
         first_factor(9, "a3")
         second_factor(8, "b0")
         second_factor(9, "b1")
-        quantize([6, 7], "a3")
+        quantize([6, 7], [(2, "a3", nc.scalar.copy)])
         first_factor(10, "a1")
         first_factor(11, "a0")
-        second_factor(10, "b2")
-        second_factor(11, "b3")
-        quantize([8, 9], "a0")
-        quantize([10], "a2", copy=nc.vector.tensor_copy)
-        quantize([11], "a1")
+        second_factor_in_halves(10, ("b2", "b0"))
+        second_factor_in_halves(11, ("b3", "b1"))
+        quantize([8, 9], [(1, "a0", nc.vector.tensor_copy), (1, "a3", nc.scalar.copy)])
+        quantize([10], [(1, "a2", nc.vector.tensor_copy)])
+        quantize([11], [(1, "a1", nc.scalar.copy)])
         routed_results([4, 5, 6, 7], "b0", nc.scalar.copy)
         routed_results([2, 3], "a3", nc.vector.tensor_copy)
         routed_results([1], "b1", nc.scalar.copy)

from contextlib import ExitStack

import concourse.mybir as mybir
from concourse.masks import make_identity

K, T, E, C, H, N = 1024, 512, 8, 128, 512, 128
FLOPS = 2 * (E * C + T) * (2 * K * H + H * N)

F32 = mybir.dt.float32
BF16 = mybir.dt.bfloat16
I32 = mybir.dt.int32
U32 = mybir.dt.uint32
U16 = mybir.dt.uint16
U8 = mybir.dt.uint8
FP8X4 = mybir.dt.float8_e4m3fn_x4
FP4X4 = mybir.dt.float4_e2m1fn_x4
MULT = mybir.AluOpType.mult
ADD = mybir.AluOpType.add
RELU = mybir.ActivationFunctionType.Relu

P = 128
PASSES = K // 512
SLOTS = E * C
SHARED = E
GATHER = 256
HALF = T // 2
QUARTERS = T // P
JOBS = QUARTERS + E
W1_GROUPS = (range(6, E + 1), range(4, 6), range(0, 4))
W3_GROUPS = (range(6, E + 1), range(3, 6), range(0, 3))
REGION = 4 * H


def load_rows(queue, plane, rows, which):
    by_row = rows.rearrange("m (q r) c -> r q m c", r=4)
    for r in which:
        queue.dma_start(out=plane[r:P:32, :, :].bitcast(I32), in_=by_row[r].bitcast(I32))


def tile_moe_shr_glu_relu_kernel(
    tc, x_words, x_scales, w1_words, w1_scales, w3_words, w3_scales, w2_words, w2_scales, gate, offs, pos1, pos2, out
):
    nc = tc.nc
    with ExitStack() as ctx:
        keep = ctx.enter_context(tc.tile_pool(name="keep", bufs=1))
        ring = ctx.enter_context(tc.tile_pool(name="ring", bufs=3))
        reuse = ctx.enter_context(tc.tile_pool(name="reuse", bufs=1))
        psum = ctx.enter_context(tc.psum_pool(name="psum", bufs=1))

        def shared_bytes(shape, dtype, name, region):
            return reuse.tile(shape, dtype, name=name, align_bytes=64, offset=region * REGION)

        def expert_of(job):
            return SHARED if job < QUARTERS else JOBS - 1 - job

        offs_t = keep.tile([P, SLOTS // 16], U16, name="offs_t")
        pos1_t = keep.tile([P, T // 16], U16, name="pos1_t")
        pos2_t = keep.tile([P, T // 16], U16, name="pos2_t")
        xw = [keep.tile([P, T], U32, name="xw%d" % o, align_bytes=64) for o in range(PASSES)]
        xs = keep.tile([P, PASSES, T], U8, name="xs", align_bytes=64)
        w1 = [keep.tile([P, 2 * PASSES, 2 * H], U8, name="w1_%d" % c, align_bytes=64) for c in range(E // 2 - 1)]
        w1.append(shared_bytes([P, 2 * PASSES, 2 * H], U8, "w1_first", JOBS + 2))
        w1_shared = shared_bytes([P, PASSES, 2 * H], U8, "w1_shared", JOBS)
        w3 = [keep.tile([P, PASSES, 2 * H], U8, name="w3_%d" % e, align_bytes=64) for e in range(E - 1)]
        w3.append(shared_bytes([P, PASSES, 2 * H], U8, "w3_first", JOBS + 4))
        w3.append(shared_bytes([P, PASSES, 2 * H], U8, "w3_shared", JOBS + 1))
        w2 = keep.tile([P, E + 1, 2 * N], U8, name="w2", align_bytes=64)
        s1 = [keep.tile([P, len(group) * PASSES, H], U8, name="s1_%d" % g, align_bytes=64) for g, group in enumerate(W1_GROUPS[:2])]
        s3 = [keep.tile([P, len(group) * PASSES, H], U8, name="s3_%d" % g, align_bytes=64) for g, group in enumerate(W3_GROUPS[:2])]
        gates = keep.tile([P, 2, T], F32, name="gates")
        gate1, gate2 = gates[:, 0, :], gates[:, 1, :]

        for plane in (xs, s1[0], s3[0], s3[1], s1[1]):
            nc.vector.memset(plane[:].bitcast(I32), 0)

        def load_words(tile, words):
            nc.sync.dma_start(out=tile[:].bitcast(I32), in_=words.rearrange("s p c -> p s c").bitcast(I32))

        def load_tokens(o):
            nc.sync.dma_start(out=xw[o][:].bitcast(I32), in_=x_words[o].rearrange("p t r -> p (t r)").bitcast(I32))

        def load_group(plane, scales, group):
            load_rows(nc.sync, plane, scales[group.start : group.stop].rearrange("e s f c -> (e s) f c"), range(4))

        def load_w1_pair(c):
            load_words(w1[c], w1_words[2 * c : 2 * c + 2].rearrange("e s p c -> (e s) p c"))

        def load_w1_single(e):
            nc.sync.dma_start(
                out=w1[e // 2][:, (e % 2) * PASSES : (e % 2 + 1) * PASSES, :].bitcast(I32),
                in_=w1_words[e].rearrange("s p c -> p s c").bitcast(I32),
            )

        load_tokens(0)
        nc.sync.dma_start(offs_t[:], offs)
        load_rows(nc.sync, xs, x_scales, range(4))
        load_words(w1_shared, w1_words[SHARED])
        load_group(s1[0], w1_scales, W1_GROUPS[0])
        load_group(s3[0], w3_scales, W3_GROUPS[0])
        load_tokens(1)
        load_words(w3[SHARED], w3_words[SHARED])
        load_w1_pair(3)
        load_words(w3[7], w3_words[7])
        load_words(w3[6], w3_words[6])
        load_w1_pair(2)
        load_words(w3[5], w3_words[5])
        load_words(w3[4], w3_words[4])

        gathered = {}

        def gather(c, o, sort, behind=None, offset=0):
            entries = offs_t[:, c * GATHER // 16 : (c + 1) * GATHER // 16]
            name = "g%s%d_%d" % (sort, c, o)
            dtype = U32 if sort == "w" else U8
            if behind is None:
                tile = keep.tile([P, GATHER], dtype, name=name, align_bytes=64)
            else:
                tile = reuse.tile([P, GATHER], dtype, name=name, align_bytes=64, offset=behind * REGION + offset)
            window = xw[o][:] if sort == "w" else xs[:, o, :]
            nc.vector.tensor_copy(tile[:], window.indirect(entries))
            gathered[(c, o, sort)] = tile

        for c in (3, 2, 1, 0):
            gather(c, 0, "w")
        for c in (3, 2):
            for o in range(PASSES):
                gather(c, o, "s")
        for c in (3, 2, 1):
            gather(c, 1, "w")
        held = {3: [(1, 0, "s"), (1, 1, "s")], 5: [(0, 1, "w"), (0, 0, "s")], 7: [(0, 1, "s")]}

        def one_pass(acc, job, o, weights, planes, groups, part=slice(0, H)):
            e = expert_of(job)
            if e == SHARED:
                cols = slice(job * P, (job + 1) * P)
                words, scales = xw[o][:, cols], xs[:, o, cols]
            else:
                cols = slice((e % 2) * C, (e % 2 + 1) * C)
                words, scales = gathered[(e // 2, o, "w")][:, cols], gathered[(e // 2, o, "s")][:, cols]
            g = [e in group for group in groups].index(True)
            nc.tensor.matmul_mx(
                out=acc[:],
                lhsT=words.bitcast(FP8X4),
                lhsT_scale=scales,
                rhs=weights[:, 2 * part.start : 2 * part.stop].bitcast(FP4X4),
                rhs_scale=planes[g][:, (e - groups[g].start) * PASSES + o, part],
                start=(o == 0),
                stop=(o == PASSES - 1),
            )

        def w1_of(job, o):
            e = expert_of(job)
            return w1_shared[:, o, :] if e == SHARED else w1[e // 2][:, (e % 2) * PASSES + o, :]

        relu_a = {}
        hidden = {}
        codes = {}

        def take_relu(job, a):
            relu_a[job] = shared_bytes([P, 2, P, 2], F32, "relu_a%d" % job, job)
            nc.scalar.activation(relu_a[job][:], a[:].rearrange("p (m u d) -> p u m d", u=2, d=2), RELU)

        def first_factor(job, bank):
            a = psum.tile([P, H], F32, name="a", tag=bank)
            for o in range(PASSES):
                one_pass(a, job, o, w1_of(job, o), s1, W1_GROUPS)
            take_relu(job, a)

        def second_factor(job, bank, behind=None):
            b = psum.tile([P, H], F32, name="b", tag=bank)
            for o in range(PASSES):
                one_pass(b, job, o, w3[expert_of(job)][:, o, :], s3, W3_GROUPS)
            if behind is None:
                hidden[job] = ring.tile([P, 2, P, 2], BF16, name="h", bufs=6)
            else:
                hidden[job] = shared_bytes([P, 2, P, 2], BF16, "h%d" % job, behind)
            nc.vector.tensor_tensor(hidden[job][:], b[:].rearrange("p (m u d) -> p u m d", u=2, d=2), relu_a[job][:], MULT)
            for i, key in enumerate(held.get(job, [])):
                gather(*key, behind=job, offset=i * REGION // 2)

        def second_factor_in_halves(job, banks):
            hidden[job] = ring.tile([P, 2, P, 2], BF16, name="h", bufs=6)
            for half, bank in enumerate(banks):
                b = psum.tile([P, H // 2], F32, name="b_half", tag=bank)
                for o in range(PASSES):
                    one_pass(b, job, o, w3[expert_of(job)][:, o, :], s3, W3_GROUPS, slice(half * H // 2, (half + 1) * H // 2))
                words = slice(half * P // 2, (half + 1) * P // 2)
                nc.vector.tensor_tensor(
                    hidden[job][:, :, words, :], b[:].rearrange("p (m u d) -> p u m d", u=2, d=2), relu_a[job][:, :, words, :], MULT
                )

        def quantize(jobs, turns):
            count = len(jobs)
            grouped = ring.tile([P, 2, P, 2], F32, name="grouped", align_bytes=64)
            done = 0
            for width, bank, copy in turns:
                turned = psum.tile([P, 2, 2, P], F32, name="turned", tag=bank)
                for i, job in enumerate(jobs[done : done + width]):
                    pairs = hidden[job][:].rearrange("p u m d -> p u (m d)").bitcast(F32)
                    for u in range(2):
                        nc.tensor.transpose(turned[:, i, u, :], pairs[:, u, :], ident[:])
                copy(grouped[:, done : done + width, :, :], turned[:, 0:width, :, :].rearrange("p j u c -> p j c u"))
                done = done + width
            words = keep.tile([P, count * P], U32, name="hq%d" % jobs[0], align_bytes=64)
            scales = keep.tile([P, count * P], U8, name="hs%d" % jobs[0], align_bytes=64)
            nc.vector.quantize_mx(
                out=words[:].bitcast(FP8X4),
                scales=scales[:],
                in_=grouped[:, 0:count, :, :].rearrange("p j c u -> p (j c u)").bitcast(BF16),
            )
            for i, job in enumerate(jobs):
                codes[job] = (words[:, i * P : (i + 1) * P], scales[:, i * P : (i + 1) * P])

        def second_layer(acc, job):
            e = expert_of(job)
            nc.tensor.matmul_mx(
                out=acc,
                lhsT=w2[:, e, :].bitcast(FP4X4),
                lhsT_scale=s2[:, e, :],
                rhs=codes[job][0].bitcast(FP8X4),
                rhs_scale=codes[job][1],
                start=True,
                stop=True,
            )

        y = keep.tile([P, SLOTS], F32, name="y")

        def routed_results(experts, bank, copy):
            acc = psum.tile([P, H], F32, name="y_acc", tag=bank)
            for i, e in enumerate(experts):
                second_layer(acc[:, i * C : (i + 1) * C], JOBS - 1 - e)
            copy(y[:, experts[0] * C : (experts[-1] + 1) * C], acc[:, 0 : len(experts) * C])

        shared_a = [psum.tile([P, H], F32, name="a", tag="a%d" % job) for job in range(QUARTERS)]
        for o in range(PASSES):
            for job in range(QUARTERS):
                one_pass(shared_a[job], job, o, w1_of(job, o), s1, W1_GROUPS)
        for job in range(QUARTERS):
            take_relu(job, shared_a[job])
        for job in range(QUARTERS):
            second_factor(job, "b%d" % job)
        ident = shared_bytes([P, P], F32, "ident", 0)
        make_identity(nc, ident[:])
        first_factor(4, "a0")
        first_factor(5, "a1")
        second_factor(4, "b0")
        second_factor(5, "b1")
        s1.append(shared_bytes([P, len(W1_GROUPS[2]) * PASSES, H], U8, "s1_2", JOBS))
        s3.append(shared_bytes([P, len(W3_GROUPS[2]) * PASSES, H], U8, "s3_2", JOBS + 2))
        s2 = shared_bytes([P, E + 1, N], U8, "s2", JOBS + 4)
        load_group(s3[1], w3_scales, W3_GROUPS[1])
        load_group(s1[1], w1_scales, W1_GROUPS[1])
        load_group(s1[2], w1_scales, W1_GROUPS[2])
        load_group(s3[2], w3_scales, W3_GROUPS[2])
        for pair in ((3, 2), (1, 0)):
            for e in pair:
                load_w1_single(e)
            for e in pair:
                load_words(w3[e], w3_words[e])
        load_words(w2, w2_words.rearrange("e s p c -> (e s) p c"))
        load_rows(nc.sync, s2, w2_scales.rearrange("e s f c -> (e s) f c"), range(4))
        nc.sync.dma_start(pos1_t[:], pos1)
        nc.sync.dma_start(pos2_t[:], pos2)
        nc.sync.dma_start(out=gates[:], in_=gate.rearrange("g p t -> p g t"))
        quantize([0, 1], [(2, "a2", nc.scalar.copy)])
        quantize([2, 3], [(2, "a3", nc.scalar.copy)])
        first_factor(6, "a0")
        first_factor(7, "a1")
        second_factor(6, "b2")
        second_factor(7, "b3")
        quantize([4, 5], [(2, "a0", nc.scalar.copy)])
        first_factor(8, "a2")
        first_factor(9, "a3")
        second_factor(8, "b0")
        second_factor(9, "b1")
        quantize([6, 7], [(2, "a3", nc.scalar.copy)])
        first_factor(10, "a1")
        first_factor(11, "a0")
        second_factor_in_halves(10, ("b2", "b0"))
        second_factor_in_halves(11, ("b3", "b1"))
        quantize([8, 9], [(1, "a0", nc.vector.tensor_copy), (1, "a3", nc.scalar.copy)])
        quantize([10], [(1, "a2", nc.vector.tensor_copy)])
        quantize([11], [(1, "a1", nc.scalar.copy)])
        routed_results([4, 5, 6, 7], "b0", nc.scalar.copy)
        routed_results([2, 3], "a3", nc.vector.tensor_copy)
        routed_results([1], "b1", nc.scalar.copy)
        routed_results([0], "a2", nc.vector.tensor_copy)
        y_shared = psum.tile([P, T], F32, name="y_shared", tag="b2")
        for job in range(QUARTERS):
            second_layer(y_shared[:, job * P : (job + 1) * P], job)

        copy_f = mybir.ActivationFunctionType.Copy
        low, high = slice(0, HALF), slice(HALF, T)
        low_entries, high_entries = slice(0, HALF // 16), slice(HALF // 16, T // 16)
        second_low = keep.tile([P, HALF], F32, name="second_low")
        first_high = keep.tile([P, HALF], F32, name="first_high")
        second_high = keep.tile([P, HALF], F32, name="second_high")
        nc.scalar.activation(second_low[:], y[:].indirect(pos2_t[:, low_entries]), copy_f)
        nc.scalar.activation(first_high[:], y[:].indirect(pos1_t[:, high_entries]), copy_f)
        for q in range(2):
            entries = pos2_t[:, (HALF + q * P) // 16 : (HALF + (q + 1) * P) // 16]
            nc.scalar.activation(second_high[:, q * P : (q + 1) * P], y[:].indirect(entries), copy_f)
        first = keep.tile([P, T], F32, name="first")
        second = keep.tile([P, T], F32, name="second")
        partial = keep.tile([P, T], F32, name="partial")
        total = keep.tile([P, T], F32, name="total")
        nc.vector.tensor_tensor(first[:, low], y[:].indirect(pos1_t[:, low_entries]), gate1[:, low], MULT)
        nc.vector.tensor_tensor(second[:, low], second_low[:], gate2[:, low], MULT)
        nc.vector.tensor_tensor(partial[:, low], y_shared[:, low], first[:, low], ADD)
        nc.vector.tensor_tensor(first[:, high], first_high[:], gate1[:, high], MULT)
        nc.vector.tensor_tensor(total[:, low], partial[:, low], second[:, low], ADD)
        nc.sync.dma_start(out=out[:, low], in_=total[:, low])
        nc.vector.tensor_tensor(partial[:, high], y_shared[:, high], first[:, high], ADD)
        quarters = [slice(HALF + q * P, HALF + (q + 1) * P) for q in range(2)]
        for q, cols in enumerate(quarters):
            nc.vector.tensor_tensor(second[:, cols], second_high[:, q * P : (q + 1) * P], gate2[:, cols], MULT)
        for cols in quarters:
            nc.vector.tensor_tensor(total[:, cols], partial[:, cols], second[:, cols], ADD)
            nc.sync.dma_start(out=out[:, cols], in_=total[:, cols])
